import numpy as np, ml_dtypes
CORES = [9,25,41,57]
N = 4
import mx_ref
BF = ml_dtypes.bfloat16
def gentries(a):
    return np.ascontiguousarray(a.reshape(8, 16, -1).transpose(0, 2, 1)).reshape(8, -1)
def gtable(e):
    e = np.asarray(e); return np.ascontiguousarray(e.reshape(8, -1, 16).transpose(0, 2, 1)).reshape(128, -1).astype(np.int32)
def gcols(t, e):
    v = np.concatenate([t.reshape(8, 16, -1, 4), np.zeros((8, 16, 1, 4), BF)], axis=2)
    return np.ascontiguousarray(np.stack([v[g][:, e[g]] for g in range(8)])).reshape(128, -1)
def gpick(z, e):
    return np.concatenate([z[16 * g:16 * g + 16][:, e[g]] for g in range(8)])
def tile(rs):
    return np.stack(rs, axis=2).reshape(128, -1).astype(BF)
def pick(q, e):
    c = np.concatenate([q[0].reshape(128, -1, 4), np.zeros((128, 1, 4), np.uint8)], axis=1); s = np.concatenate([q[1], np.ones((16, 1), np.uint8)], axis=1)
    return (np.ascontiguousarray(c[:, e].reshape(128, -1)), np.ascontiguousarray(s[:, e]))
def join(*qs):
    return (np.concatenate([q[0] for q in qs], axis=1), np.concatenate([q[1] for q in qs], axis=1))
def put(q, e, v):
    c, s = q[0].reshape(128, -1, 4).copy(), q[1].copy(); c[:, e] = v[0].reshape(128, -1, 4); s[:, e] = v[1]
    return (c.reshape(128, -1), s)
def pk(c, s):
    return (np.ascontiguousarray(c), mx_ref.live(s))
def emit(q):
    return q[0], q[1]
def packed(v, rng):
    q = [mx_ref.quantize(np.ascontiguousarray(v[r])) for r in range(N)]
    return np.stack([a for a, b in q]), np.stack([mx_ref.plane(b, rng) for a, b in q])
def values_of_codes():
    e, c = np.zeros((128, 128, 4), np.float32), np.zeros((128, 2, 4), np.uint8)
    e[np.arange(128), np.arange(128), 0] = 1
    c[:127, :, 0] = np.arange(256).reshape(2, 128).T[:127]
    return mx_ref.matmul(mx_ref.quantize(e.reshape(128, 512).astype(BF)), (c.reshape(128, 8), np.full((16, 2), 127, np.uint8))).T.reshape(-1).astype(np.float64)
CODE_VALUE, SCALE_VALUE = values_of_codes(), 2.0 ** (np.arange(256) - 127.0)
def decode(q):
    return (CODE_VALUE[q[0]].reshape(16, 8, -1, 4) * SCALE_VALUE[q[1]][:, None, :, None] + 0.0).reshape(128, -1).astype(np.float32)
def f(rng, *shape):
    return mx_ref.flush((rng.standard_normal(shape, dtype=np.float32) * np.exp2(rng.integers(-2, 3, shape[:-1] + (1,)))).astype(BF))
def wide(rng, *shape, cols=0):
    v = rng.standard_normal(shape, dtype=np.float32) * np.exp2(rng.integers(-12, 13, shape)).astype(np.float32)
    if cols: v *= np.repeat(np.exp2(rng.integers(-cols, cols + 1, shape[:-2] + (1, shape[-1] // 4))) * (rng.random(shape[:-2] + (1, shape[-1] // 4)) > 0.0625), 4, axis=-1).astype(np.float32)
    return mx_ref.flush(v.astype(BF))
C = 384
STEP = [1, 2, 3]
GROUP, PLACE = np.arange(8)[:, None], np.arange(C)
def numbers_of(rng):
    return {"x": np.array(f(rng, N, 128, 4 * C)), "u": np.array(f(rng, N, 128, 512)), "v": np.array(f(rng, N, 128, 512))}
def orders(rng):
    return rng.permuted(np.tile(np.arange(C), (N, 8, 1)), axis=2)
def paired(e):
    k = np.zeros_like(e)
    np.put_along_axis(k, e[:, :, 0::2], e[:, :, 1::2], 2)
    np.put_along_axis(k, e[:, :, 1::2], e[:, :, 0::2], 2)
    return k
def stored(p, q, mu):
    return {a: np.stack([gtable(k[r]) for r in range(N)]) for a, k in (("pl", p), ("ql", q), ("ml", mu))}
def lists(rng):
    return stored(paired(orders(rng)), paired(orders(rng)), paired(orders(rng)))
def layers(rng, still=[]):
    w = np.array(f(rng, N, 128, 2048)).reshape(N, 8, 16, 4, 8, 16, 4)
    for i in still:
        w[:, :, i] = 0
        w[:, :, :, :, :, i] = 0
    return w
def weights(rng, w):
    c, s = packed(np.ascontiguousarray(w).reshape(N, 128, 2048), rng)
    return {"wc": c, "ws": s}
def setup_inputs(rng):
    return {**numbers_of(rng), **lists(rng), **weights(rng, layers(rng))}
def setup_inputs_ties(rng):
    d = numbers_of(rng)
    e = orders(rng)
    mu = paired(orders(rng))
    k = np.zeros((N, 8, C))
    for r in range(N):
        h = rng.permutation(8)
        c = rng.integers(0, C, 2)
        k[r, h[1], min(c[0], mu[r, h[1], c[0]])] = -1
        k[r, h[2], max(c[1], mu[r, h[2], c[1]])] = -1
        k[r, h[3], e[r, h[3], :2]] = -1
        k[r, h[4]] = rng.integers(-4, 0, C)
        k[r, h[5]] = rng.integers(-1, 3, C)
        k[r, h[6]] = rng.integers(1, 4, C)
        k[r, h[7]] = rng.integers(0, 2, C)
        k[r, h[7], e[r, h[7], 0]] = -1
        k[r, h[7], e[r, h[7], 2 * rng.integers(1, C // 2)]] = -1
    x = d["x"].reshape(N, 8, 16, C, 4)
    x[:, :, 0] = 0
    x[:, :, 0, :, 0] = k.astype(np.float32).astype(BF)
    u = d["u"].reshape(N, 128, 128, 4)
    u[:, :, ::16] = 0
    for h in range(0, 128, 16): u[:, h, h, 0] = 1
    return {"x": x.reshape(N, 128, 4 * C), "u": u.reshape(N, 128, 512), "v": d["v"], **stored(paired(e), paired(np.roll(e, -1, axis=2)), mu), **weights(rng, layers(rng, [0]))}
def setup_inputs_near(rng):
    d = numbers_of(rng)
    x = d["x"].astype(np.float32).reshape(N, 8, 16, C, 4)
    x[:, :, :2] = 0
    x[:, :, 8:] = 0
    x[:, :, 1, :, 0] = rng.choice([-1.0, 1.0], (N, 8, C)) * (1.0 + 0.125 * rng.integers(0, 8, (N, 8, C))) * 2.0 ** -7
    u = d["u"].reshape(N, 128, 128, 4)
    u[:, :, ::16] = 0
    w = layers(rng, [0, 1, 8, 9, 10, 11, 12, 13, 14, 15])
    o = rng.permutation(N) % 4
    for r in range(N):
        c = rng.choice([-1.0, 1.0], (8, 1))
        s = rng.integers(0, 16, (8, C))
        digits = ((s[:, :, None] >> np.arange(4)) & 1) * np.exp2(np.arange(4) - 23.0)
        if o[r] < 2:
            x[r, :, 0, :, 0] = c
            x[r, :, 8] = digits
            x[r, :, 11, :, 0] = 2.0 ** -10
        elif o[r] == 2: x[r, :, 8] = digits * rng.choice([-1.0, 1.0], (8, C, 1))
        else:
            x[r, :, 8, :, 0] = np.where(s < 8, 1.25, 0.0) * 2.0 ** -29 * c
            x[r, :, 9, :, 0] = np.where(s < 8, 0.0, 1.125) * 2.0 ** -29 * c
            x[r, :, 12, :, 0] = 2.0 ** -28
            for g in range(8): w[r, g, 1, 0, g, 10, 0] = 2.0 ** -30
            for i, g in enumerate(rng.permutation(8)[:4]):
                if i < 2:
                    e = rng.choice([-1.0, 1.0], C) * 2.0 ** -29
                    x[r, g, 8, :, 0] = 1.25 * e
                    x[r, g, 9, :, 0] = -1.125 * e
                else:
                    x[r, g, 8:] = 0
                    x[r, g, 12, :, 0] = 2.0 ** -30
                    w[r, g, 1, 0, g, 10, 0] = -2.0 ** -30
                    w[r, g, 1, 0, g, 11, 0] = 2.0 ** -30
        at = [0, C - 1, int(rng.integers(C)), int(rng.integers(C))]
        for g, j in zip(rng.permutation(8)[:4], at): x[r, g, 0, j, 0] = 2.0 ** 29 * rng.choice([-1.0, 1.0])
        k = 1.0 if o[r] == 0 else 2.0 ** -30
        for h in range(0, 128, 16):
            u[r, h, h, 0] = k if o[r] < 2 else 1.0
            if o[r] < 2: u[r, h + 11, h, 0] = k
            if o[r] < 3: u[r, h + 8, h] = k
            else:
                u[r, h + 8, h, 0] = k
                u[r, h + 9, h, 0] = 1.125 * k
                u[r, h + 10, h, 0] = k
                u[r, h + 11, h, 0] = 1.125 * k
    return {"x": x.reshape(N, 128, 4 * C).astype(BF), "u": u.reshape(N, 128, 512), "v": d["v"], **lists(rng), **weights(rng, w)}
def setup_inputs_odd(rng):
    d = numbers_of(rng)
    x = (1.0 + (2 * rng.integers(0, 64, (N, 16, 8, C, 4)) + 1) * 2.0 ** -7) * np.exp2(-rng.integers(0, 7, (N, 16, 8, C, 4)).astype(np.float64)) * rng.choice([-1.0, 1.0], (N, 16, 8, C, 4))
    x[:, :, 0, :, 0] = 1.96875 * 2.0 ** 8 * rng.choice([-1.0, 1.0], (N, 16, C))
    x[:, 1::2, 0, :, 0] *= np.where(rng.random((N, 8, C)) < 0.5, 2.0 ** -6, 1.0)
    u = d["u"].reshape(N, 16, 8, 128, 4)
    u[:, :, 0, ::16] = 0
    for r in range(N):
        for i, g in enumerate(rng.permutation(8)[:4]):
            x[r, 2 * g, 1, :, 0] = (8 + rng.integers(0, 2, C)) * 2.0 ** (i - 8)
            u[r, :, :, 16 * g] = 0
            u[r, 2 * g, 1, 16 * g, 0] = 1.0
    return {"x": x.astype(np.float32).reshape(N, 128, 4 * C).astype(BF), "u": u.reshape(N, 128, 512), "v": d["v"], **lists(rng), **weights(rng, layers(rng, [0, 8]))}
def setup_inputs_ends(rng):
    d = numbers_of(rng)
    o, e = rng.permutation(N) % 2, rng.permutation(N) % 4
    sign = rng.choice([-1.0, 1.0], (128, 1, 4))
    half = np.repeat(rng.choice([0.5, 1.0], (N, 1, C, 2)), 2, axis=3)
    small = sign * (1.0 + 0.125 * rng.integers(0, 8, (N, 128, C, 4))) * 2.0 ** -30
    x = sign * half * (14 + rng.integers(0, 3, (N, 128, C, 4))) * 2.0 ** 26
    x[o == 1] = small[o == 1]
    x[:, 112:120] = sign[112:120]
    x[:, 120:] = small[:, 120:]
    size = np.where(o == 0, 2.0 ** 30, 2.0 ** -30)
    kinds = np.array([[1, 1, 1, 1]] * 2 + [[-1, -1, -1, -1]] * 3 + [[1, 1, -1, -1]] * 2 + [[0, 0, 0, 0]])
    u = d["u"].astype(np.float32).reshape(N, 128, 128, 4)
    for r in range(N): u[r, :, ::16] = sign * kinds[rng.permutation(8)][None] * size[r]
    u[:, 112:, ::16] = 0
    v = rng.choice([-1.0, 1.0], (N, 128, 512)) * size[:, None, None]
    a = orders(rng)
    p, q, mu = paired(a), paired(np.roll(a, -1, axis=2)), paired(orders(rng))
    q[e == 1] = p[e == 1]
    mu[e == 1] = p[e == 1]
    p[e == 2] = C - 1 - np.arange(C)
    q[e == 2] = np.arange(C) ^ 1
    q[e == 3] = paired(orders(rng))[e == 3]
    w = np.zeros((N, 128, 4, 128, 4), np.float32)
    i, n = np.arange(112), np.arange(8)
    for b in range(4):
        for r in range(N):
            if o[r] == 0: w[r, i, b, i, b] = -4.0
            w[r, (120 if b < 2 else 96) + n, b, 112 + n, b] = 2.0 ** 30 if b < 2 else 2.0 ** -30
    return {"x": x.astype(np.float32).reshape(N, 128, 4 * C).astype(BF), "u": u.reshape(N, 128, 512).astype(BF), "v": v.astype(np.float32).astype(BF), **stored(p, q, mu), **weights(rng, w.astype(BF))}
def setup_inputs_spread(rng):
    d = setup_inputs(rng)
    d["x"] = wide(rng, N, 128, 4 * C, cols=6)
    return d
def check_inputs(d):
    b = []
    for k in ("x", "u", "v"):
        a = np.abs(d[k].astype(np.float32))
        if not (np.isfinite(a).all() and ((a == 0) | (a >= 2.0 ** -30) & (a <= 2.0 ** 30)).all()): b.append("a value of " + k)
    for k in ("pl", "ql", "ml"):
        for r in range(N):
            e = gentries(d[k][r])
            if not ((e >= 0) & (e < C)).all(): b.append("an entry of " + k)
            elif (e == PLACE).any() or (e[GROUP, e] != PLACE).any(): b.append(k + ": no involution without fixed points")
    none, least, most = [emit(mx_ref.quantize(np.full((128, 16), k, np.float32).astype(BF)))[1][0, 0] for k in (0.0, 2.0 ** -30, 2.0 ** 30)]
    for r in range(N):
        if ((d["wc"][r] == 0x7F) | (d["wc"][r] == 0xFF)).any(): b.append("wc: a code that is no number")
        s = mx_ref.live(d["ws"][r])
        if ((s != none) & ((s < least) | (s > most))).any(): b.append("ws: a scale out of range")
        if (((d["wc"][r].reshape(16, 8, 512, 4) & 0x7F) != 0) & (s == none)[:, None, :, None]).any(): b.append("wc: a code other than zero under the scale of zeros")
    return b
def powers(a):
    k = [np.tile(PLACE, (8, 1))]
    for i in range(C // 2 - 1): k.append(a[GROUP, k[-1]])
    return np.stack(k)
def mirror(p, q, stop):
    ahead, back = powers(q[GROUP, p]), powers(p[GROUP, q])
    i, j = np.argmax(stop[GROUP, ahead], axis=0), np.argmax(stop[GROUP, back], axis=0)
    return ahead[i, GROUP, back[j, GROUP, PLACE]]
def reference(x, u, v, pl, ql, ml, wc, ws):
    qu = [mx_ref.quantize(u[r]) for r in range(N)]
    lay = [pk(wc[r], ws[r]) for r in range(N)]
    p, q, mu = [[gentries(a[r]).astype(np.int64) for r in range(N)] for a in (pl, ql, ml)]
    now = [x[r] for r in range(N)]
    for step in STEP:
        own, sent, image = [], [], []
        for r in range(N):
            t = mx_ref.quantize(now[r])
            s = mx_ref.matmul(qu[r], t)[::16] + np.float32(0.0)
            d = decode(t).astype(BF)
            m = mirror(p[r], q[r], s < 0)
            z = (gcols(d, m).astype(np.float32) + gcols(d, q[r][GROUP, p[r]]).astype(np.float32)) * np.float32(0.5)
            sent.append(mx_ref.quantize(z.astype(BF)))
            w = (PLACE < mu[r]) & (s[GROUP, m] > s[GROUP, m[GROUP, mu[r]]])
            e = np.where(w | w[GROUP, mu[r]], mu[r], PLACE)
            q[r] = e[GROUP, q[r][GROUP, e]]
            own.append(d)
            image.append(m)
        now = [tile([gpick(mx_ref.matmul(pick(lay[r], np.arange(128 * b, 128 * b + 128)), sent[r ^ step]) * np.float32(0.03125), image[r]) + own[r][:, b::4].astype(np.float32) for b in range(4)]) for r in range(N)]
    y, qo = np.zeros((N, 128, C), np.float32), np.zeros((N, 8, C), np.float32)
    oc, osc = np.zeros((N, 128, 4 * C), np.uint8), np.zeros((N, 16, C), np.uint8)
    for r in range(N):
        t = mx_ref.quantize(now[r])
        y[r] = mx_ref.matmul(mx_ref.quantize(v[r]), t)
        qo[r] = q[r]
        oc[r], osc[r] = emit(t)
    return {"y": y, "qo": qo, "oc": oc, "osc": osc}

@@ -1,0 +1,437 @@
+from concourse.mybir import dt, AluOpType as OP, ActivationFunctionType as AF
+
+C = 384
+SCRATCH = {}
+LISTS = ["qw", "pw", "muw", "mupw", "sgw", "uw", "ix0", "ix1", "ix2"] + ["l%d" % n for n in (2, 4, 8, 16, 32, 64)] + ["a%d" % s for s in (1, 2, 3)] + ["m%d" % s for s in (1, 2, 3)] + ["ra%d" % s for s in (1, 2, 3)] + ["rm%d" % s for s in (1, 2, 3)]
+
+
+def _sb(names, width, dtype, where="sbuf"):
+    for n in names.split():
+        SCRATCH[n] = (where, [128, width], dtype)
+
+
+_sb("iot murow mpr ssb smr spr dr sgp sgr cv0 cv1 k32 ysb qr0 qr1 qr2 qr3", C, "float32")
+_sb("wlo wmid", 8 * C, "float32")
+_sb("wtop", 6 * C, "float32")
+_sb("rsb", 4 * C, "float32")
+_sb("mk0 mk1 sc0 sc1 blk16 k16 u16 sg16", C, "float16")
+_sb("mask hf hm h0 h1 hd blkb", C, "bfloat16")
+_sb("hs gs th2 tg2", 416, "bfloat16")
+_sb("th1 tg1", C, "bfloat16")
+_sb("x0 xn z fo fp fa", 4 * C, "bfloat16")
+_sb("ut vt ones", 512, "bfloat16")
+_sb("et", 2048, "bfloat16")
+_sb("eq wq", 512, "float8_e4m3fn_x4")
+_sb("es wsc", 512, "uint8")
+_sb("uq vq up", 128, "float8_e4m3fn_x4")
+_sb("us vs ups", 128, "uint8")
+_sb("tq0 tq1 tq2 tq3 lq1 lq2 lq3 zq1 zq2 zq3", C, "float8_e4m3fn_x4")
+_sb("ts0 ts1 ts2 ts3 lp1 lp2 lp3 zs1 zs2 zs3", C, "uint8")
+_sb("pli qli mli", 24, "int32")
+_sb("ij idi", C, "int32")
+_sb("pi qi", 8, "int32")
+_sb("c24i u8i", 24, "int32")
+_sb("cols", 8, "float32")
+_sb("uoff", 8, "uint16")
+AT = {}
+
+
+def _wrapped(buf, names, dtype):
+    names = names.split()
+    for i, n in enumerate(names):
+        AT[n] = (buf, 24 * i)
+    _sb(buf, 24 * len(names), dtype)
+
+
+_wrapped("wi", "ei d2i d1i d0i", "int32")
+_wrapped("wf", "cw pf mupf ww ep eq0 ep2 eq2 ev ne neg nw cur n3 d2f d2g d1f d0f if0 if1 if2 dd du dz dw dsg pmc", "float32")
+_wrapped("wl", " ".join(n for n in LISTS if n[0] != "r"), "uint16")
+_wrapped("wr", " ".join(n for n in LISTS if n[0] == "r"), "uint16")
+_sb("pa pb", 2048, "float32", "psum")
+DMAS = ["dpl", "dql", "dml", "dx", "du_", "dv", "dwc", "dws", "doc", "dos0", "dos1", "dos2", "dos3", "dy", "dqo"]
+SEMAPHORES = ["sv", "sa", "st", "sp", "ls"] + ["%s%d" % (k, s) for s in (1, 2, 3) for k in ("at", "aa", "am")] + DMAS
+
+
+def rank_program(g, core, T, topo):
+    rank = T.rank_of(core)
+    if rank is None:
+        return
+    queue = {"v": g.vector, "a": g.scalar, "t": g.tensor, "p": g, "s": g.sync}
+    count = {"sv": 0, "sa": 0, "st": 0, "sp": 0}
+    own = {"v": "sv", "a": "sa", "t": "st", "p": "sp"}
+    know = {q: {} for q in queue}
+    then = {}
+    writer, readers = {}, {}
+
+    def merge(a, b):
+        for k, v in b.items():
+            if a.get(k, 0) < v:
+                a[k] = v
+
+    def meets(name, part, table):
+        d = table.get(name, {})
+        return [d[k] for k in d if part is None or k is None or k == part]
+
+    def regs(xs):
+        return [(x, None) if not isinstance(x, tuple) else x for x in xs]
+
+    def waits(q, reads, writes):
+        need = {}
+        for n, p in reads + writes:
+            for tok in meets(n, p, writer):
+                need[tok[0]] = max(need.get(tok[0], 0), tok[1])
+        for n, p in writes:
+            for toks in meets(n, p, readers):
+                for tok in toks:
+                    need[tok[0]] = max(need.get(tok[0], 0), tok[1])
+        for s in sorted(need):
+            if know[q].get(s, 0) < need[s]:
+                queue[q].wait_ge(T.sem[s], need[s])
+                know[q][s] = need[s]
+                merge(know[q], then.get((s, need[s]), {}))
+
+    def note(tok, reads, writes):
+        for n, p in reads:
+            readers.setdefault(n, {}).setdefault(p, []).append(tok)
+        for n, p in writes:
+            w = writer.setdefault(n, {})
+            r = readers.setdefault(n, {})
+            if p is None:
+                w.clear()
+                r.clear()
+            r[p] = []
+            w[p] = tok
+
+    def op(q, reads, writes, call, *args, **kw):
+        reads, writes = regs(reads), regs(writes)
+        waits(q, reads, writes)
+        s = own[q]
+        count[s] += 1
+        then[(s, count[s])] = dict(know[q])
+        call(*args, **kw).then_inc(T.sem[s], 1)
+        note((s, count[s]), reads, writes)
+
+    def dma(q, sem, out, in_, reads, writes):
+        reads, writes = regs(reads), regs(writes)
+        waits(q, reads, writes)
+        count[sem] = 16
+        then[(sem, 16)] = dict(know[q])
+        queue[q].dma_start(out, in_).then_inc(T.sem[sem], 16)
+        note((sem, 16), reads, writes)
+
+    V, A, P, M = g.vector, g.scalar, g, g.tensor
+
+    def sl(n, i=None, w=C):
+        if n in AT:
+            buf, o = AT[n]
+            return T[buf][:, o:o + 24]
+        return T[n][:, :] if i is None else T[n][:, w * i:w * i + w]
+
+    def gath(out, oreg, win, wreg, lst):
+        op("a", [wreg, lst], [oreg], A.activation, out, win.indirect(sl(lst)), AF.Copy)
+
+    def copy_a(out, reads, writes, in_, **kw):
+        op("a", reads, writes, A.activation, out, in_, kw.pop("func", AF.Copy), **kw)
+
+    turn = [0]
+
+    def masked(win, wreg, lst):
+        i = turn[0] = 1 - turn[0]
+        mk, sc = "mk%d" % i, "sc%d" % i
+        op("v", [wreg, lst, "mask"], [mk], V.tensor_tensor, sl(mk), win.indirect(sl(lst)), sl("mask"), OP.mult)
+        op("v", [mk, "blk16"], [sc], V.tensor_tensor_scan, sl(sc), sl("blk16"), sl(mk), 0.0, OP.mult, OP.add)
+        return T[sc][:, 15:C:16], sc
+
+    def rowlist(row, rreg, lst, k="k32", cv="cv"):
+        i = turn[0] = 1 - turn[0]
+        cv = "%s%d" % (cv, i)
+        op("v", [rreg, k], [cv], V.tensor_tensor_scan, sl(cv), sl(k), row, 0.0, OP.add, OP.min)
+        op("v", [cv, ("cols", 0)], [lst], V.tensor_scalar, sl(lst), T[cv][:, 15:C:16], T.cols[:, 0:1], None, OP.add)
+
+    def small(out, in0, op0, in1):
+        op("v", [in0, in1], [out], V.tensor_tensor, sl(out), sl(in0), sl(in1), op0)
+
+    def ts(out, in0, s1, s2, o0, o1, reads, writes):
+        if o1 is None:
+            op("v", reads, writes, V.tensor_scalar, out, in0, s1, None, o0)
+        else:
+            op("v", reads, writes, V.tensor_scalar, out, in0, s1, s2, o0, o1)
+
+    def ts1(out, in0, s1, o0):
+        op("v", [in0], [out], V.tensor_scalar, sl(out), sl(in0), s1, None, o0)
+
+    def vcopy(out, in_):
+        op("v", [in_], [out], V.tensor_copy, sl(out), sl(in_))
+
+    def mm(out, oreg, lq, lqs, a, rq, rs):
+        op("t", [lq, lqs, rq, rs], [oreg], M.matmul_mx, out, T[lq][:, a:a + 128], T[lqs][:, a:a + 128], sl(rq), sl(rs), True, True)
+
+    dma("s", "dpl", sl("pli"), T.pl[:, :], [], ["pli"])
+    dma("a", "dx", sl("x0"), T.x[:, :], [], ["x0"])
+    dma("s", "dql", sl("qli"), T.ql[:, :], [], ["qli"])
+    dma("s", "du_", sl("ut"), T.u[:, :], [], ["ut"])
+    dma("s", "dml", sl("mli"), T.ml[:, :], [], ["mli"])
+    dma("s", "dwc", T.wq[:, :].bitcast(dt.uint8), T.wc[:, :], [], ["wq"])
+    dma("s", "dws", sl("wsc"), T.ws[:, :], [], ["wsc"])
+    dma("s", "dv", sl("vt"), T.v[:, :], [], ["vt"])
+
+    op("p", [], ["iot"], P.iota, sl("iot"), [[1, C]], 0, 0, allow_small_or_imprecise_dtypes=True)
+    op("p", [], ["pi"], P.iota, T.pi[:, 0:1], [[1, 1]], 0, 1)
+    op("p", [], ["ij"], P.iota, sl("ij"), [[1, C]], 128, -1)
+    op("p", [], ["u8i"], P.iota, T.u8i[:, 0:8], [[16, 8]], 0, 0)
+    op("p", [], ["c24i"], P.iota, sl("c24i"), [[16, 24]], 0, 0)
+    op("p", [], ["blkb"], P.iota, sl("blkb"), [[0, 24], [1, 16]], 0, 0, allow_small_or_imprecise_dtypes=True)
+    op("p", [], ["ones"], P.iota, sl("ones"), [[0, 512]], 1, 0, allow_small_or_imprecise_dtypes=True)
+    for b in range(4):
+        op("p", ["ones"], [("et", b)], P.affine_select, sl("et", b, 512), sl("ones"), [[-1, 512]], OP.is_equal, 0.0, b, 4)
+    ts(T.qi[:, 0:1], T.pi[:, 0:1], 15, None, OP.bitwise_and, None, ["pi"], [("qi", 0)])
+    ts(T.cols[:, 0:1], T.qi[:, 0:1], 15, 1024.0, OP.is_lt, OP.mult, [("qi", 0)], [("cols", 0)])
+    ts1("idi", "ij", 15, OP.bitwise_and)
+    ts(sl("cv0"), sl("idi"), 0, 2048.0, OP.is_equal, OP.mult, ["idi"], ["cv0"])
+    ts(sl("cv1"), sl("idi"), 1, -1024.0, OP.is_equal, OP.mult, ["idi"], ["cv1"])
+    op("v", ["cv0", "cv1"], ["k32"], V.tensor_tensor, sl("k32"), sl("cv0"), sl("cv1"), OP.add)
+    vcopy("pw", "pli")
+    vcopy("qw", "qli")
+    gath(sl("qr0"), "qr0", sl("iot"), "iot", "qw")
+    gath(T.wlo[:, C:2 * C], ("wlo", 1), sl("qr0"), "qr0", "pw")
+    op("v", ["u8i"], ["uoff"], V.tensor_copy, sl("uoff"), T.u8i[:, 0:8])
+    op("v", ["ut"], ["uq", "us"], V.quantize_mx, sl("uq"), sl("us"), sl("ut"))
+    op("v", ["uq", "uoff"], ["up"], V.tensor_copy, T.up[:, :].bitcast(dt.uint32), T.uq[:, :].bitcast(dt.uint32).indirect(T.uoff[:, :]))
+    op("v", ["us", "uoff"], ["ups"], V.tensor_copy, sl("ups"), T.us[:, :].indirect(T.uoff[:, :]))
+    ts(T.qi[:, 1:2], T.pi[:, 0:1], 31, None, OP.bitwise_and, None, ["pi"], [("qi", 1)])
+    ts(T.cols[:, 1:2], T.qi[:, 0:1], 8, 256.0, OP.is_lt, OP.mult, [("qi", 0)], [("cols", 1)])
+    ts(T.cols[:, 2:3], T.qi[:, 0:1], 8, 256.0, OP.is_ge, OP.mult, [("qi", 0)], [("cols", 2)])
+
+    def rest_a():
+        ts(T.cols[:, 3:4], T.qi[:, 1:2], 16, None, OP.is_lt, None, [("qi", 1)], [("cols", 3)])
+        ts(T.cols[:, 4:5], T.qi[:, 1:2], 16, None, OP.is_ge, None, [("qi", 1)], [("cols", 4)])
+        ts(T.cols[:, 5:6], T.qi[:, 0:1], 0, None, OP.add, None, [("qi", 0)], [("cols", 5)])
+        ts(sl("cw"), sl("c24i"), T.cols[:, 5:6], None, OP.add, None, ["c24i", ("cols", 5)], ["cw"])
+        vcopy("pf", "pli")
+        small("pmc", "pf", OP.subtract, "cw")
+        ts1("mask", "idi", 0, OP.is_equal)
+        ts1("blk16", "blkb", 0.0, OP.is_gt)
+        op("v", [], [("hs", 1)], V.memset, T.hs[:, 0:16], 0.0)
+        op("v", [], [("hs", 2)], V.memset, T.hs[:, 400:416], 0.0)
+        op("v", [], [("gs", 1)], V.memset, T.gs[:, 0:16], 0.0)
+        op("v", [], [("gs", 2)], V.memset, T.gs[:, 400:416], 0.0)
+
+    def rest_b():
+        vcopy("k16", "k32")
+        rowlist(sl("mpr"), "mpr", "mupf")
+        vcopy("mupw", "mupf")
+        small("ww", "mupf", OP.subtract, "pf")
+        op("v", ["vt"], ["vq", "vs"], V.quantize_mx, sl("vq"), sl("vs"), sl("vt"))
+
+    slot = {0: ("wlo", 0)}
+    for n in range(1, 8):
+        slot[n] = ("wlo", n)
+        slot[8 * n] = ("wmid", n)
+    slot[64], slot[128], slot["p"], slot["p64"], slot["p128"] = [("wtop", i) for i in (1, 2, 3, 4, 5)]
+
+    def row(n):
+        w, i = slot[n]
+        return T[w][:, i * C:i * C + C]
+
+    def lname(s, n):
+        return "a%d" % s if n == 1 else "l%d" % n
+
+    def power(s, to, n, by):
+        gath(row(to), slot[to], row(n), slot[n], lname(s, by))
+
+    def start_rows():
+        for w in ("wlo", "wmid", "wtop"):
+            copy_a(T[w][:, 0:C], ["iot"], [(w, 0)], sl("iot"))
+        gath(row("p"), slot["p"], sl("iot"), "iot", "pw")
+
+    def chain_row(s, i):
+        power(s, 2 << i, 1 << i, 1 << i)
+
+    def chain_list(s, i):
+        rowlist(row(2 << i), slot[2 << i], lname(s, 2 << i))
+
+    send_n = [0]
+
+    def send(s, dst, sem, out, in_, reads):
+        waits("p", regs(reads), [])
+        rid, pid, _ = topo.addr(dst)
+        mask = topo.mask(core, dst)
+        g.remote_dma(out, in_, T.sem[sem], T.sem.ls, pid, rid, mask)
+        send_n[0] += len(topo.engines(core, dst))
+
+    steps = T.tables["STEP"] if "STEP" in T.tables else [1, 2, 3]
+    cores = T.cores
+    for s in (1, 2, 3):
+        dst = cores[rank ^ steps[s - 1]]
+        ne = len(topo.engines(core, dst))
+        tq, tsn = "tq%d" % (s - 1), "ts%d" % (s - 1)
+        xin = "x0" if s == 1 else "xn"
+        mw, rm, ra = "m%d" % s, "rm%d" % s, "ra%d" % s
+        op("v", [xin], [tq, tsn], V.quantize_mx, sl(tq), sl(tsn), sl(xin))
+        mm(T.pb[:, 0:C], ("pb", 0), "up", "ups", 0, tq, tsn)
+        send(s, dst, "at%d" % s, T["lq%d" % s][:, :].bitcast(dt.uint8), T[tq][:, :].bitcast(dt.uint8), [tq])
+        send(s, dst, "at%d" % s, sl("lp%d" % s), sl(tsn), [tsn])
+        if s == 1:
+            rowlist(row(1), slot[1], "a1")
+            chain_row(1, 0)
+            start_rows()
+        send(s, dst, "aa%d" % s, sl(ra), sl("a%d" % s), ["a%d" % s])
+        for tok, names in ((("at%d" % s, 2 * ne), ["lq%d" % s, "lp%d" % s]), (("aa%d" % s, ne), [ra]), (("am%d" % s, ne), [rm])):
+            count[tok[0]] = tok[1]
+            note(tok, [], regs(names))
+        if s > 1:
+            chain_list(s, 0)
+        ts(sl("hm"), T.pb[:, 0:C], 0.0, T.cols[:, 2:3], OP.is_ge, OP.mult, [("cols", 2)], ["hm", ("pb", 0)])
+        ts(sl("hf"), T.pb[:, 0:C], 0.0, T.cols[:, 1:2], OP.is_ge, OP.mult, [("cols", 1)], ["hf", ("pb", 0)])
+        if s == 1:
+            chain_list(s, 0)
+            rest_a()
+            op("v", ["et"], ["eq", "es"], V.quantize_mx, sl("eq"), sl("es"), sl("et"))
+        op("v", ["hm", "pw", "hf"], ["h0"], V.tensor_tensor, sl("h0"), T.hm[:, :].indirect(sl("pw")), sl("hf"), OP.add)
+        for b in range(4):
+            mm(T.pa[:, 512 * b:512 * b + C], ("pa", b), "eq", "es", 128 * b, tq, tsn)
+        for b in range(4):
+            mm(T.pb[:, 512 * b:512 * b + C], ("pb", b), "eq", "es", 128 * b, "lq%d" % s, "lp%d" % s) if b else None
+        jobs = [(0, lambda: copy_a(sl("ssb"), [], ["ssb", ("pb", 0)], T.pb[:, 0:C]))]
+        for b in range(2):
+            jobs.append((0, lambda b=b: copy_a(sl("fo", b), [], [("fo", b), ("pa", b)], T.pa[:, 512 * b:512 * b + C])))
+        jobs.append((1, lambda: power(s, 3, 1, 2)))
+        jobs += [(2, lambda n=n: power(s, n + 4, n, 4)) for n in (1, 2, 3)]
+        jobs.append((4, lambda: power(s, 24, 8, 16)))
+        for b in range(2, 4):
+            jobs.append((0, lambda b=b: copy_a(sl("fo", b), [], [("fo", b), ("pa", b)], T.pa[:, 512 * b:512 * b + C])))
+        if s == 1:
+            jobs += [(5, lambda: vcopy("muw", "mli")), (5, lambda: gath(sl("murow"), "murow", sl("iot"), "iot", "muw")), (5, lambda: gath(sl("mpr"), "mpr", sl("murow"), "murow", "pw"))]
+        jobs += [(5, lambda n=n: power(s, n + 32, n, 32)) for n in (8, 16, 24)]
+        jobs += [(6, lambda: power(s, 128, 64, 64)), (6, lambda: power(s, "p64", "p", 64)), (6, lambda: power(s, "p128", "p64", 64))]
+
+        def some(i, k):
+            while jobs and k and jobs[0][0] <= i:
+                jobs.pop(0)[1]()
+                k -= 1
+
+        cur = "h0"
+        for i, n in enumerate((1, 2, 4, 8, 16, 32, 64, 64)):
+            if i < 5:
+                chain_row(s, i + 1)
+            some(i, 2 if i < 2 else 1)
+            nxt = "h1" if cur == "h0" else "h0"
+            oreg, out = (nxt, sl(nxt)) if i < 7 else (("hs", 0), T.hs[:, 16:16 + C])
+            ts(sl("hd"), sl(cur), float(-n), None, OP.add, None, [cur], ["hd"])
+            op("v", [cur, lname(s, n), "hd"], [oreg], V.tensor_tensor, out, T[cur][:, :].indirect(sl(lname(s, n))), sl("hd"), OP.min)
+            if i < 5:
+                chain_list(s, i + 1)
+            cur = nxt
+        gath(T.gs[:, 16:16 + C], ("gs", 0), T.hs[:, 16:16 + C], "hs", "pw")
+        op("v", ["hs"], ["th1"], V.transpose, sl("th1"), T.hs[:, 16:16 + C])
+        op("v", ["hs"], ["th2"], V.transpose, sl("th2"), sl("hs"))
+        some(9, 99)
+        mm(T.pb[:, 0:C], ("pb", 0), "eq", "es", 0, "lq%d" % s, "lp%d" % s)
+        op("v", ["gs"], ["tg1"], V.transpose, sl("tg1"), T.gs[:, 16:16 + C])
+        op("v", ["gs"], ["tg2"], V.transpose, sl("tg2"), sl("gs"))
+        for out, k, a, a0, a1, b, b0, b1 in (("ep", 0, "th1", 0, 384, "tg1", 8, 384), ("eq0", 1, "th1", 16, 384, "tg1", 24, 384), ("eq0", 0, "th2", 16, 400, "tg2", 24, 400), ("ep", 1, "th2", 32, 416, "tg2", 40, 416)):
+            op("v", [a, b], [(out, k)], V.tensor_tensor, T[AT[out][0]][:, AT[out][1] + k:AT[out][1] + 24:2], T[a][:, a0:a1:32], T[b][:, b0:b1:32], OP.subtract)
+        ts(sl("ep2"), sl("ep"), T.cols[:, 3:4], None, OP.mult, None, ["ep", ("cols", 3)], ["ep2"])
+        ts(sl("eq2"), sl("eq0"), T.cols[:, 4:5], None, OP.mult, None, ["eq0", ("cols", 4)], ["eq2"])
+        small("ev", "ep2", OP.add, "eq2")
+        ts1("ne", "ev", -1.0, OP.mult)
+        ts1("neg", "ev", 0.0, OP.is_lt)
+        small("ei", "ev", OP.max, "ne")
+        small("nw", "neg", OP.mult, "pmc")
+        ts1("d0i", "ei", 7, OP.bitwise_and)
+        small("cur", "nw", OP.add, "cw")
+        ts1("d0f", "d0i", 384, OP.mult)
+        ts1("d1i", "ei", 56, OP.bitwise_and)
+        small("if0", "d0f", OP.add, "cur")
+        ts1("d2i", "ei", 192, OP.bitwise_and)
+        vcopy("ix0", "if0")
+        ts1("d1f", "d1i", 48, OP.mult)
+        ts1("d2f", "d2i", 6, OP.mult)
+        ts1("n3", "neg", 1152.0, OP.mult)
+        small("d2g", "d2f", OP.add, "n3")
+        for k, (w, dig) in enumerate((("wlo", "d1f"), ("wmid", "d2g"), ("wtop", None))):
+            r, rr = masked(sl(w), w, "ix%d" % k)
+            if dig:
+                op("v", [rr, dig], ["if%d" % (k + 1)], V.tensor_tensor, sl("if%d" % (k + 1)), r, sl(dig), OP.add)
+                vcopy("ix%d" % (k + 1), "if%d" % (k + 1))
+            else:
+                op("v", [rr], [mw], V.tensor_copy, sl(mw), r)
+        send(s, dst, "am%d" % s, sl(rm), sl(mw), [mw])
+        for b in range(4):
+            copy_a(sl("fp", b), [], [("fp", b), ("pb", b)], T.pb[:, 512 * b:512 * b + C], scale=0.5)
+        if s == 1:
+            rest_b()
+        qr, zq, zs = "qr%d" % (s - 1), "zq%d" % s, "zs%d" % s
+
+        def half(b):
+            gath(sl("fa", b), ("fa", b), sl("fp", b), ("fp", b), ra)
+
+        def zpart(b):
+            op("v", [("fp", b), rm, ("fa", b)], [("z", b)], V.tensor_tensor, T.z[:, b:4 * C:4], sl("fp", b).indirect(sl(rm)), sl("fa", b), OP.add)
+
+        def sigma():
+            rowlist(sl("sg16"), "sg16", "dd", "k16", "sc")
+            small("du", "dd", OP.mult, "ww")
+            ts1("dz", "du", 0.0, OP.is_lt)
+            small("dw", "dz", OP.mult, "ww")
+            small("dsg", "dw", OP.add, "pf")
+            vcopy("sgw", "dsg")
+
+        gath(sl("smr"), "smr", sl("ssb"), "ssb", mw)
+        gath(sl("spr"), "spr", sl("smr"), "smr", "pw")
+        half(0)
+        op("v", ["smr", "mupw", "spr"], ["dr"], V.tensor_tensor, sl("dr"), T.smr[:, :].indirect(sl("mupw")), sl("spr"), OP.subtract)
+        copy_a(sl("sg16"), ["dr"], ["sg16"], sl("dr"), func=AF.Sign)
+        half(1)
+        zpart(0)
+        if s < 3:
+            sigma()
+            gath(sl("u16"), "u16", sl(qr), qr, "sgw")
+            half(2)
+            zpart(1)
+            rowlist(sl("u16"), "u16", "uw", "k16", "sc")
+            half(3)
+            gath(sl("sgp"), "sgp", sl("iot"), "iot", "sgw")
+            gath(sl("sgr"), "sgr", sl("sgp"), "sgp", "pw")
+        else:
+            half(2)
+            zpart(1)
+            half(3)
+        zpart(2)
+        zpart(3)
+        op("v", ["z"], [zq, zs], V.quantize_mx, sl(zq), sl(zs), sl("z"))
+        for b in range(4):
+            mm(T.pa[:, 512 * b:512 * b + C], ("pa", b), "wq", "wsc", 128 * b, zq, zs)
+        if s < 3:
+            gath(row(1), slot[1], sl("sgr"), "sgr", "uw")
+        else:
+            sigma()
+        for b in range(4):
+            copy_a(sl("rsb", b), [], [("rsb", b), ("pa", b)], T.pa[:, 512 * b:512 * b + C], scale=0.03125)
+            if b == 2 and s < 3:
+                rowlist(row(1), slot[1], "a%d" % (s + 1))
+                chain_row(s + 1, 0)
+        if s == 3:
+            gath(sl("u16"), "u16", sl(qr), qr, "sgw")
+            gath(sl("sgp"), "sgp", sl("iot"), "iot", "sgw")
+            gath(sl("sgr"), "sgr", sl("sgp"), "sgp", "pw")
+        else:
+            gath(sl("qr%d" % s), "qr%d" % s, row(1), slot[1], "pw")
+        for b in range(4):
+            op("v", [("rsb", b), mw, ("fo", b)], [("xn", b)], V.tensor_tensor, T.xn[:, b:4 * C:4], sl("rsb", b).indirect(sl(mw)), sl("fo", b), OP.add)
+            if s == 3 and b == 2:
+                rowlist(sl("u16"), "u16", "uw", "k16", "sc")
+                gath(row(1), slot[1], sl("sgr"), "sgr", "uw")
+    op("v", ["xn"], ["tq3", "ts3"], V.quantize_mx, sl("tq3"), sl("ts3"), sl("xn"))
+    mm(T.pb[:, 0:C], ("pb", 0), "vq", "vs", 0, "tq3", "ts3")
+    dma("s", "doc", T.oc[:, :], T.tq3[:, :].bitcast(dt.uint8), ["tq3"], [])
+    copy_a(sl("ysb"), [], ["ysb", ("pb", 0)], T.pb[:, 0:C])
+    dma("a", "dy", T.y[:, :], sl("ysb"), ["ysb"], [])
+    gath(sl("qr3"), "qr3", row(1), slot[1], "pw")
+    for k in range(4):
+        dma("s", "dos%d" % k, T.osc[4 * k:4 * k + 4, 0:C], T.ts3[32 * k:32 * k + 4, 0:C], ["ts3"], [])
+    dma("s", "dqo", T.qo[:, :], T.qr3[0:128:16, :], ["qr3"], [])
+    for sem in sorted(count):
+        if know["p"].get(sem, 0) < count[sem]:
+            g.wait_ge(T.sem[sem], count[sem])
+    g.wait_ge(T.sem.ls, send_n[0])

@@ -1,8 +1,9 @@
 from concourse.mybir import dt, AluOpType as OP, ActivationFunctionType as AF
 
 C = 384
+HD = (1, 2, 3)
 SCRATCH = {}
-LISTS = ["qw", "pw", "muw", "mupw", "sgw", "uw", "ix0", "ix1", "ix2"] + ["l%d" % n for n in (2, 4, 8, 16, 32, 64)] + ["a%d" % s for s in (1, 2, 3)] + ["m%d" % s for s in (1, 2, 3)] + ["ra%d" % s for s in (1, 2, 3)] + ["rm%d" % s for s in (1, 2, 3)]
+LISTS = ["qw", "pw", "muw", "mupw", "sgw", "uw", "ix0", "ix1", "ix2", "ix3"] + ["l%d" % n for n in (2, 4, 8, 16, 32, 64)] + ["a%d" % s for s in (1, 2, 3)] + ["m%d" % s for s in (1, 2, 3)] + ["ra%d" % s for s in (1, 2, 3)] + ["rm%d" % s for s in (1, 2, 3)]
 
 
 def _sb(names, width, dtype, where="sbuf"):
@@ -10,12 +11,13 @@ def _sb(names, width, dtype, where="sbuf"):
         SCRATCH[n] = (where, [128, width], dtype)
 
 
-_sb("iot murow mpr ssb smr spr dr sgp sgr cv0 cv1 k32 ysb qr0 qr1 qr2 qr3", C, "float32")
-_sb("wlo wmid", 8 * C, "float32")
-_sb("wtop", 6 * C, "float32")
+_sb("iot murow mpr sgp sgr u16 sg16 qr0 qr1 qr2", C, "bfloat16")
+_sb("wlo wmi whi", 4 * 512, "bfloat16")
+_sb("wtop", 7 * 512, "bfloat16")
+_sb("ssb smr spr dr ysb qr3", C, "float32")
 _sb("rsb", 4 * C, "float32")
-_sb("mk0 mk1 sc0 sc1 blk16 k16 u16 sg16", C, "float16")
-_sb("mask hf hm h0 h1 hd blkb", C, "bfloat16")
+_sb("mk0 mk1 sc0 sc1 k16 ka kb", C, "float16")
+_sb("hf hm h0 h1 hd", C, "bfloat16")
 _sb("hs gs th2 tg2", 416, "bfloat16")
 _sb("th1 tg1", C, "bfloat16")
 _sb("x0 xn z fo fp fa", 4 * C, "bfloat16")
@@ -43,12 +45,12 @@ def _wrapped(buf, names, dtype):
     _sb(buf, 24 * len(names), dtype)
 
 
-_wrapped("wi", "ei d2i d1i d0i", "int32")
-_wrapped("wf", "cw pf mupf ww ep eq0 ep2 eq2 ev ne neg nw cur n3 d2f d2g d1f d0f if0 if1 if2 dd du dz dw dsg pmc", "float32")
+_wrapped("wi", "ei ex d3i d2i d1i d0i", "int32")
+_wrapped("wf", "cw pf mupf ww ep eq0 ep2 eq2 ev ne ng nw cur tgt if0 if1 if2 if3 dd du dz dw dsg pmc", "float32")
 _wrapped("wl", " ".join(n for n in LISTS if n[0] != "r"), "uint16")
 _wrapped("wr", " ".join(n for n in LISTS if n[0] == "r"), "uint16")
 _sb("pa pb", 2048, "float32", "psum")
-DMAS = ["dpl", "dql", "dml", "dx", "du_", "dv", "dwc", "dws", "doc", "dos0", "dos1", "dos2", "dos3", "dy", "dqo"]
+DMAS = ["dpl", "dql", "dml", "dx", "du_", "dv", "dwc", "dws", "doc", "dos0", "dos1", "dos2", "dos3", "dy0", "dy1", "dqo", "gap_wlo", "gap_wmi", "gap_whi", "gap_wtop"] + ["id%d" % i for i in range(5)]
 SEMAPHORES = ["sv", "sa", "st", "sp", "ls"] + ["%s%d" % (k, s) for s in (1, 2, 3) for k in ("at", "aa", "am")] + DMAS
 
 
@@ -113,11 +115,12 @@ def rank_program(g, core, T, topo):
 
     def dma(q, sem, out, in_, reads, writes):
         reads, writes = regs(reads), regs(writes)
-        waits(q, reads, writes)
-        count[sem] = 16
-        then[(sem, 16)] = dict(know[q])
+        if sem not in count:
+            waits(q, reads, writes)
+        count[sem] = n = count.get(sem, 0) + 16
+        then[(sem, n)] = dict(know[q])
         queue[q].dma_start(out, in_).then_inc(T.sem[sem], 16)
-        note((sem, 16), reads, writes)
+        note((sem, n), reads, writes)
 
     V, A, P, M = g.vector, g.scalar, g, g.tensor
 
@@ -130,23 +133,33 @@ def rank_program(g, core, T, topo):
     def gath(out, oreg, win, wreg, lst):
         op("a", [wreg, lst], [oreg], A.activation, out, win.indirect(sl(lst)), AF.Copy)
 
-    def copy_a(out, reads, writes, in_, **kw):
-        op("a", reads, writes, A.activation, out, in_, kw.pop("func", AF.Copy), **kw)
+    def both(out, win, lst):
+        buf, o = AT[lst]
+        op("v", [win, lst], [(out, 0)], V.tensor_copy, T[out][:, 0:C // 2], sl(win).indirect(T[buf][:, o:o + 12]))
+        op("a", [win, lst], [(out, 1)], A.activation, T[out][:, C // 2:C], sl(win).indirect(T[buf][:, o + 12:o + 24]), AF.Copy)
+
+    def copy_a(out, reads, writes, in_, func=AF.Copy, **kw):
+        op("a", reads, writes, A.activation, out, in_, func, **kw)
 
     turn = [0]
 
-    def masked(win, wreg, lst):
+    def rowlist(row, rreg, lst, col=0):
+        i = turn[0] = 1 - turn[0]
+        cv = "sc%d" % i
+        op("v", [rreg, "k16"], [cv], V.tensor_tensor_scan, sl(cv), sl("k16"), row, 0.0, OP.add, OP.min)
+        op("v", [cv, ("cols", col)], [lst], V.tensor_scalar, sl(lst), T[cv][:, 15:C:16], T.cols[:, col:col + 1], None, OP.add)
+
+    def level(win, lst, out, dig):
         i = turn[0] = 1 - turn[0]
         mk, sc = "mk%d" % i, "sc%d" % i
-        op("v", [wreg, lst, "mask"], [mk], V.tensor_tensor, sl(mk), win.indirect(sl(lst)), sl("mask"), OP.mult)
-        op("v", [mk, "blk16"], [sc], V.tensor_tensor_scan, sl(sc), sl("blk16"), sl(mk), 0.0, OP.mult, OP.add)
-        return T[sc][:, 15:C:16], sc
-
-    def rowlist(row, rreg, lst, k="k32", cv="cv"):
-        i = turn[0] = 1 - turn[0]
-        cv = "%s%d" % (cv, i)
-        op("v", [rreg, k], [cv], V.tensor_tensor_scan, sl(cv), sl(k), row, 0.0, OP.add, OP.min)
-        op("v", [cv, ("cols", 0)], [lst], V.tensor_scalar, sl(lst), T[cv][:, 15:C:16], T.cols[:, 0:1], None, OP.add)
+        both(mk, win, lst)
+        op("v", [mk, "k16"], [sc], V.tensor_tensor_scan, sl(sc), sl("k16"), sl(mk), 0.0, OP.add, OP.min)
+        if dig:
+            f = "if%s" % out[-1]
+            op("v", [sc, dig], [f], V.tensor_tensor, sl(f), T[sc][:, 15:C:16], sl(dig), OP.add)
+            op("v", [f, ("cols", 0)], [out], V.tensor_scalar, sl(out), sl(f), T.cols[:, 0:1], None, OP.add)
+        else:
+            op("v", [sc, ("cols", 0)], [out], V.tensor_scalar, sl(out), T[sc][:, 15:C:16], T.cols[:, 0:1], None, OP.add)
 
     def small(out, in0, op0, in1):
         op("v", [in0, in1], [out], V.tensor_tensor, sl(out), sl(in0), sl(in1), op0)
@@ -170,30 +183,37 @@ def rank_program(g, core, T, topo):
     dma("a", "dx", sl("x0"), T.x[:, :], [], ["x0"])
     dma("s", "dql", sl("qli"), T.ql[:, :], [], ["qli"])
     dma("s", "du_", sl("ut"), T.u[:, :], [], ["ut"])
+    waits("s", [("x0", None)], [])
     dma("s", "dml", sl("mli"), T.ml[:, :], [], ["mli"])
     dma("s", "dwc", T.wq[:, :].bitcast(dt.uint8), T.wc[:, :], [], ["wq"])
     dma("s", "dws", sl("wsc"), T.ws[:, :], [], ["wsc"])
     dma("s", "dv", sl("vt"), T.v[:, :], [], ["vt"])
 
-    op("p", [], ["iot"], P.iota, sl("iot"), [[1, C]], 0, 0, allow_small_or_imprecise_dtypes=True)
     op("p", [], ["pi"], P.iota, T.pi[:, 0:1], [[1, 1]], 0, 1)
     op("p", [], ["ij"], P.iota, sl("ij"), [[1, C]], 128, -1)
+    op("p", [], ["iot"], P.iota, sl("iot"), [[1, C]], -192, 0, allow_small_or_imprecise_dtypes=True)
     op("p", [], ["u8i"], P.iota, T.u8i[:, 0:8], [[16, 8]], 0, 0)
     op("p", [], ["c24i"], P.iota, sl("c24i"), [[16, 24]], 0, 0)
-    op("p", [], ["blkb"], P.iota, sl("blkb"), [[0, 24], [1, 16]], 0, 0, allow_small_or_imprecise_dtypes=True)
     op("p", [], ["ones"], P.iota, sl("ones"), [[0, 512]], 1, 0, allow_small_or_imprecise_dtypes=True)
+    for i, (w, j) in enumerate((("wlo", 0), ("wmi", 0), ("whi", 0), ("wtop", 0), ("wtop", 3))):
+        dma("s", "id%d" % i, T[w][:, j * 512:j * 512 + C], sl("iot"), ["iot"], [(w, j)])
+    for w, n in (("wlo", 4), ("wmi", 4), ("whi", 4), ("wtop", 7)):
+        for j in range(n):
+            dma("s", "gap_" + w, T[w][:, j * 512 + C:j * 512 + 512], T.ones[:, 0:128], ["ones"], [(w, "gap")])
     for b in range(4):
         op("p", ["ones"], [("et", b)], P.affine_select, sl("et", b, 512), sl("ones"), [[-1, 512]], OP.is_equal, 0.0, b, 4)
     ts(T.qi[:, 0:1], T.pi[:, 0:1], 15, None, OP.bitwise_and, None, ["pi"], [("qi", 0)])
-    ts(T.cols[:, 0:1], T.qi[:, 0:1], 15, 1024.0, OP.is_lt, OP.mult, [("qi", 0)], [("cols", 0)])
+    ts(T.cols[:, 6:7], T.qi[:, 0:1], 15, 1024.0, OP.is_lt, OP.mult, [("qi", 0)], [("cols", 6)])
+    ts(T.cols[:, 0:1], T.cols[:, 6:7], 192.0, None, OP.add, None, [("cols", 6)], [("cols", 0)])
     ts1("idi", "ij", 15, OP.bitwise_and)
-    ts(sl("cv0"), sl("idi"), 0, 2048.0, OP.is_equal, OP.mult, ["idi"], ["cv0"])
-    ts(sl("cv1"), sl("idi"), 1, -1024.0, OP.is_equal, OP.mult, ["idi"], ["cv1"])
-    op("v", ["cv0", "cv1"], ["k32"], V.tensor_tensor, sl("k32"), sl("cv0"), sl("cv1"), OP.add)
+    ts(sl("ka"), sl("idi"), 0, 2048.0, OP.is_equal, OP.mult, ["idi"], ["ka"])
     vcopy("pw", "pli")
     vcopy("qw", "qli")
     gath(sl("qr0"), "qr0", sl("iot"), "iot", "qw")
-    gath(T.wlo[:, C:2 * C], ("wlo", 1), sl("qr0"), "qr0", "pw")
+    gath(T.wlo[:, 512:512 + C], ("wlo", 1), sl("qr0"), "qr0", "pw")
+    gath(T.wtop[:, 2048:2048 + C], ("wtop", 4), sl("iot"), "iot", "pw")
+    ts(sl("kb"), sl("idi"), 1, -1024.0, OP.is_equal, OP.mult, ["idi"], ["kb"])
+    small("k16", "ka", OP.add, "kb")
     op("v", ["u8i"], ["uoff"], V.tensor_copy, sl("uoff"), T.u8i[:, 0:8])
     op("v", ["ut"], ["uq", "us"], V.quantize_mx, sl("uq"), sl("us"), sl("ut"))
     op("v", ["uq", "uoff"], ["up"], V.tensor_copy, T.up[:, :].bitcast(dt.uint32), T.uq[:, :].bitcast(dt.uint32).indirect(T.uoff[:, :]))
@@ -202,47 +222,43 @@ def rank_program(g, core, T, topo):
     ts(T.cols[:, 1:2], T.qi[:, 0:1], 8, 256.0, OP.is_lt, OP.mult, [("qi", 0)], [("cols", 1)])
     ts(T.cols[:, 2:3], T.qi[:, 0:1], 8, 256.0, OP.is_ge, OP.mult, [("qi", 0)], [("cols", 2)])
 
-    def rest_a():
-        ts(T.cols[:, 3:4], T.qi[:, 1:2], 16, None, OP.is_lt, None, [("qi", 1)], [("cols", 3)])
-        ts(T.cols[:, 4:5], T.qi[:, 1:2], 16, None, OP.is_ge, None, [("qi", 1)], [("cols", 4)])
+    def rest_v():
+        ts(T.cols[:, 3:4], T.qi[:, 1:2], 16, 512.0, OP.is_lt, OP.mult, [("qi", 1)], [("cols", 3)])
+        ts(T.cols[:, 4:5], T.qi[:, 1:2], 16, 512.0, OP.is_ge, OP.mult, [("qi", 1)], [("cols", 4)])
         ts(T.cols[:, 5:6], T.qi[:, 0:1], 0, None, OP.add, None, [("qi", 0)], [("cols", 5)])
         ts(sl("cw"), sl("c24i"), T.cols[:, 5:6], None, OP.add, None, ["c24i", ("cols", 5)], ["cw"])
         vcopy("pf", "pli")
         small("pmc", "pf", OP.subtract, "cw")
-        ts1("mask", "idi", 0, OP.is_equal)
-        ts1("blk16", "blkb", 0.0, OP.is_gt)
+        ts1("pmc", "pmc", 2.0 ** -17, OP.mult)
         op("v", [], [("hs", 1)], V.memset, T.hs[:, 0:16], 0.0)
         op("v", [], [("hs", 2)], V.memset, T.hs[:, 400:416], 0.0)
         op("v", [], [("gs", 1)], V.memset, T.gs[:, 0:16], 0.0)
         op("v", [], [("gs", 2)], V.memset, T.gs[:, 400:416], 0.0)
+        vcopy("muw", "mli")
 
     def rest_b():
-        vcopy("k16", "k32")
         rowlist(sl("mpr"), "mpr", "mupf")
         vcopy("mupw", "mupf")
         small("ww", "mupf", OP.subtract, "pf")
+        ts(sl("du"), sl("ww"), 0.0, 2.0, OP.is_lt, OP.mult, ["ww"], ["du"])
+        ts1("dd", "du", -1.0, OP.add)
+        ts(sl("tgt"), sl("dd"), T.cols[:, 6:7], None, OP.subtract, None, ["dd", ("cols", 6)], ["tgt"])
         op("v", ["vt"], ["vq", "vs"], V.quantize_mx, sl("vq"), sl("vs"), sl("vt"))
 
-    slot = {0: ("wlo", 0)}
-    for n in range(1, 8):
-        slot[n] = ("wlo", n)
-        slot[8 * n] = ("wmid", n)
-    slot[64], slot[128], slot["p"], slot["p64"], slot["p128"] = [("wtop", i) for i in (1, 2, 3, 4, 5)]
+    slot = {}
+    for n in (1, 2, 3):
+        slot[n], slot[4 * n], slot[16 * n] = ("wlo", n), ("wmi", n), ("whi", n)
+    slot[64], slot[128], slot["p"], slot["p64"], slot["p128"] = [("wtop", i) for i in (1, 2, 4, 5, 6)]
 
     def row(n):
         w, i = slot[n]
-        return T[w][:, i * C:i * C + C]
+        return T[w][:, 512 * i:512 * i + C]
 
     def lname(s, n):
         return "a%d" % s if n == 1 else "l%d" % n
 
     def power(s, to, n, by):
         gath(row(to), slot[to], row(n), slot[n], lname(s, by))
-
-    def start_rows():
-        for w in ("wlo", "wmid", "wtop"):
-            copy_a(T[w][:, 0:C], ["iot"], [(w, 0)], sl("iot"))
-        gath(row("p"), slot["p"], sl("iot"), "iot", "pw")
 
     def chain_row(s, i):
         power(s, 2 << i, 1 << i, 1 << i)
@@ -255,28 +271,25 @@ def rank_program(g, core, T, topo):
     def send(s, dst, sem, out, in_, reads):
         waits("p", regs(reads), [])
         rid, pid, _ = topo.addr(dst)
-        mask = topo.mask(core, dst)
-        g.remote_dma(out, in_, T.sem[sem], T.sem.ls, pid, rid, mask)
+        g.remote_dma(out, in_, T.sem[sem], T.sem.ls, pid, rid, topo.mask(core, dst))
         send_n[0] += len(topo.engines(core, dst))
 
     steps = T.tables["STEP"] if "STEP" in T.tables else [1, 2, 3]
-    cores = T.cores
     for s in (1, 2, 3):
-        dst = cores[rank ^ steps[s - 1]]
+        dst = T.cores[rank ^ steps[s - 1]]
         ne = len(topo.engines(core, dst))
-        tq, tsn = "tq%d" % (s - 1), "ts%d" % (s - 1)
+        tq, tsn, lq, lp = "tq%d" % (s - 1), "ts%d" % (s - 1), "lq%d" % s, "lp%d" % s
         xin = "x0" if s == 1 else "xn"
         mw, rm, ra = "m%d" % s, "rm%d" % s, "ra%d" % s
         op("v", [xin], [tq, tsn], V.quantize_mx, sl(tq), sl(tsn), sl(xin))
         mm(T.pb[:, 0:C], ("pb", 0), "up", "ups", 0, tq, tsn)
-        send(s, dst, "at%d" % s, T["lq%d" % s][:, :].bitcast(dt.uint8), T[tq][:, :].bitcast(dt.uint8), [tq])
-        send(s, dst, "at%d" % s, sl("lp%d" % s), sl(tsn), [tsn])
+        send(s, dst, "at%d" % s, T[lq][:, :].bitcast(dt.uint8), T[tq][:, :].bitcast(dt.uint8), [tq])
+        send(s, dst, "at%d" % s, sl(lp), sl(tsn), [tsn])
         if s == 1:
             rowlist(row(1), slot[1], "a1")
             chain_row(1, 0)
-            start_rows()
         send(s, dst, "aa%d" % s, sl(ra), sl("a%d" % s), ["a%d" % s])
-        for tok, names in ((("at%d" % s, 2 * ne), ["lq%d" % s, "lp%d" % s]), (("aa%d" % s, ne), [ra]), (("am%d" % s, ne), [rm])):
+        for tok, names in ((("at%d" % s, 2 * ne), [lq, lp]), (("aa%d" % s, ne), [ra]), (("am%d" % s, ne), [rm])):
             count[tok[0]] = tok[1]
             note(tok, [], regs(names))
         if s > 1:
@@ -285,25 +298,28 @@ def rank_program(g, core, T, topo):
         ts(sl("hf"), T.pb[:, 0:C], 0.0, T.cols[:, 1:2], OP.is_ge, OP.mult, [("cols", 1)], ["hf", ("pb", 0)])
         if s == 1:
             chain_list(s, 0)
-            rest_a()
-            op("v", ["et"], ["eq", "es"], V.quantize_mx, sl("eq"), sl("es"), sl("et"))
         op("v", ["hm", "pw", "hf"], ["h0"], V.tensor_tensor, sl("h0"), T.hm[:, :].indirect(sl("pw")), sl("hf"), OP.add)
-        for b in range(4):
-            mm(T.pa[:, 512 * b:512 * b + C], ("pa", b), "eq", "es", 128 * b, tq, tsn)
-        for b in range(4):
-            mm(T.pb[:, 512 * b:512 * b + C], ("pb", b), "eq", "es", 128 * b, "lq%d" % s, "lp%d" % s) if b else None
+
+        def unpack():
+            for b in range(4):
+                mm(T.pa[:, 512 * b:512 * b + C], ("pa", b), "eq", "es", 128 * b, tq, tsn)
+            for b in range(1, 4):
+                mm(T.pb[:, 512 * b:512 * b + C], ("pb", b), "eq", "es", 128 * b, lq, lp)
+
         jobs = [(0, lambda: copy_a(sl("ssb"), [], ["ssb", ("pb", 0)], T.pb[:, 0:C]))]
-        for b in range(2):
-            jobs.append((0, lambda b=b: copy_a(sl("fo", b), [], [("fo", b), ("pa", b)], T.pa[:, 512 * b:512 * b + C])))
-        jobs.append((1, lambda: power(s, 3, 1, 2)))
-        jobs += [(2, lambda n=n: power(s, n + 4, n, 4)) for n in (1, 2, 3)]
-        jobs.append((4, lambda: power(s, 24, 8, 16)))
-        for b in range(2, 4):
-            jobs.append((0, lambda b=b: copy_a(sl("fo", b), [], [("fo", b), ("pa", b)], T.pa[:, 512 * b:512 * b + C])))
         if s == 1:
-            jobs += [(5, lambda: vcopy("muw", "mli")), (5, lambda: gath(sl("murow"), "murow", sl("iot"), "iot", "muw")), (5, lambda: gath(sl("mpr"), "mpr", sl("murow"), "murow", "pw"))]
-        jobs += [(5, lambda n=n: power(s, n + 32, n, 32)) for n in (8, 16, 24)]
-        jobs += [(6, lambda: power(s, 128, 64, 64)), (6, lambda: power(s, "p64", "p", 64)), (6, lambda: power(s, "p128", "p64", 64))]
+            jobs.append((1, rest_v))
+            jobs.append((2, lambda: op("v", ["et"], ["eq", "es"], V.quantize_mx, sl("eq"), sl("es"), sl("et"))))
+            jobs.append((2, unpack))
+            jobs.append((3, lambda: gath(sl("murow"), "murow", sl("iot"), "iot", "muw")))
+            jobs.append((4, lambda: gath(sl("mpr"), "mpr", sl("murow"), "murow", "pw")))
+        else:
+            unpack()
+        jobs.append((3, lambda: power(s, 3, 1, 2)))
+        jobs.append((4, lambda: power(s, 12, 4, 8)))
+        for b in range(4):
+            jobs.append((5, lambda b=b: copy_a(sl("fo", b), [], [("fo", b), ("pa", b)], T.pa[:, 512 * b:512 * b + C])))
+        jobs += [(5, lambda: power(s, 48, 16, 32)), (6, lambda: power(s, 128, 64, 64)), (6, lambda: power(s, "p64", "p", 64))]
 
         def some(i, k):
             while jobs and k and jobs[0][0] <= i:
@@ -312,21 +328,28 @@ def rank_program(g, core, T, topo):
 
         cur = "h0"
         for i, n in enumerate((1, 2, 4, 8, 16, 32, 64, 64)):
+            if i in HD:
+                copy_a(sl("hd"), [cur], ["hd"], sl(cur), bias=float(-n))
+            else:
+                ts(sl("hd"), sl(cur), float(-n), None, OP.add, None, [cur], ["hd"])
             if i < 5:
                 chain_row(s, i + 1)
-            some(i, 2 if i < 2 else 1)
+            some(i, (1, 3, 3, 1, 1, 2, 2, 2)[i])
             nxt = "h1" if cur == "h0" else "h0"
             oreg, out = (nxt, sl(nxt)) if i < 7 else (("hs", 0), T.hs[:, 16:16 + C])
-            ts(sl("hd"), sl(cur), float(-n), None, OP.add, None, [cur], ["hd"])
             op("v", [cur, lname(s, n), "hd"], [oreg], V.tensor_tensor, out, T[cur][:, :].indirect(sl(lname(s, n))), sl("hd"), OP.min)
             if i < 5:
                 chain_list(s, i + 1)
             cur = nxt
+
+        def pback(b):
+            copy_a(sl("fp", b), [], [("fp", b), ("pb", b)], T.pb[:, 512 * b:512 * b + C], scale=0.5)
+
         gath(T.gs[:, 16:16 + C], ("gs", 0), T.hs[:, 16:16 + C], "hs", "pw")
         op("v", ["hs"], ["th1"], V.transpose, sl("th1"), T.hs[:, 16:16 + C])
         op("v", ["hs"], ["th2"], V.transpose, sl("th2"), sl("hs"))
         some(9, 99)
-        mm(T.pb[:, 0:C], ("pb", 0), "eq", "es", 0, "lq%d" % s, "lp%d" % s)
+        mm(T.pb[:, 0:C], ("pb", 0), "eq", "es", 0, lq, lp)
         op("v", ["gs"], ["tg1"], V.transpose, sl("tg1"), T.gs[:, 16:16 + C])
         op("v", ["gs"], ["tg2"], V.transpose, sl("tg2"), sl("gs"))
         for out, k, a, a0, a1, b, b0, b1 in (("ep", 0, "th1", 0, 384, "tg1", 8, 384), ("eq0", 1, "th1", 16, 384, "tg1", 24, 384), ("eq0", 0, "th2", 16, 400, "tg2", 24, 400), ("ep", 1, "th2", 32, 416, "tg2", 40, 416)):
@@ -335,30 +358,26 @@ def rank_program(g, core, T, topo):
         ts(sl("eq2"), sl("eq0"), T.cols[:, 4:5], None, OP.mult, None, ["eq0", ("cols", 4)], ["eq2"])
         small("ev", "ep2", OP.add, "eq2")
         ts1("ne", "ev", -1.0, OP.mult)
-        ts1("neg", "ev", 0.0, OP.is_lt)
+        ts(sl("ng"), sl("ev"), 0.0, 131072.0, OP.is_lt, OP.mult, ["ev"], ["ng"])
         small("ei", "ev", OP.max, "ne")
-        small("nw", "neg", OP.mult, "pmc")
-        ts1("d0i", "ei", 7, OP.bitwise_and)
+        small("nw", "ng", OP.mult, "pmc")
+        ts1("d0i", "ei", 1536, OP.bitwise_and)
         small("cur", "nw", OP.add, "cw")
-        ts1("d0f", "d0i", 384, OP.mult)
-        ts1("d1i", "ei", 56, OP.bitwise_and)
-        small("if0", "d0f", OP.add, "cur")
-        ts1("d2i", "ei", 192, OP.bitwise_and)
+        ts(sl("d1i"), sl("ei"), 2, 1536, OP.logical_shift_right, OP.bitwise_and, ["ei"], ["d1i"])
+        small("if0", "d0i", OP.add, "cur")
+        ts(sl("d2i"), sl("ei"), 4, 1536, OP.logical_shift_right, OP.bitwise_and, ["ei"], ["d2i"])
         vcopy("ix0", "if0")
-        ts1("d1f", "d1i", 48, OP.mult)
-        ts1("d2f", "d2i", 6, OP.mult)
-        ts1("n3", "neg", 1152.0, OP.mult)
-        small("d2g", "d2f", OP.add, "n3")
-        for k, (w, dig) in enumerate((("wlo", "d1f"), ("wmid", "d2g"), ("wtop", None))):
-            r, rr = masked(sl(w), w, "ix%d" % k)
-            if dig:
-                op("v", [rr, dig], ["if%d" % (k + 1)], V.tensor_tensor, sl("if%d" % (k + 1)), r, sl(dig), OP.add)
-                vcopy("ix%d" % (k + 1), "if%d" % (k + 1))
-            else:
-                op("v", [rr], [mw], V.tensor_copy, sl(mw), r)
+        level("wlo", "ix0", "ix1", "d1i")
+        power(s, "p128", "p64", 64)
+        small("ex", "ei", OP.add, "ng")
+        level("wmi", "ix1", "ix2", "d2i")
+        pback(0)
+        ts(sl("d3i"), sl("ex"), 6, 3584, OP.logical_shift_right, OP.bitwise_and, ["ex"], ["d3i"])
+        level("whi", "ix2", "ix3", "d3i")
+        pback(1)
+        level("wtop", "ix3", mw, None)
         send(s, dst, "am%d" % s, sl(rm), sl(mw), [mw])
-        for b in range(4):
-            copy_a(sl("fp", b), [], [("fp", b), ("pb", b)], T.pb[:, 512 * b:512 * b + C], scale=0.5)
+        pback(2)
         if s == 1:
             rest_b()
         qr, zq, zs = "qr%d" % (s - 1), "zq%d" % s, "zs%d" % s
@@ -370,30 +389,33 @@ def rank_program(g, core, T, topo):
             op("v", [("fp", b), rm, ("fa", b)], [("z", b)], V.tensor_tensor, T.z[:, b:4 * C:4], sl("fp", b).indirect(sl(rm)), sl("fa", b), OP.add)
 
         def sigma():
-            rowlist(sl("sg16"), "sg16", "dd", "k16", "sc")
-            small("du", "dd", OP.mult, "ww")
-            ts1("dz", "du", 0.0, OP.is_lt)
+            i = turn[0] = 1 - turn[0]
+            cv = "sc%d" % i
+            op("v", ["sg16", "k16"], [cv], V.tensor_tensor_scan, sl(cv), sl("k16"), sl("sg16"), 0.0, OP.add, OP.min)
+            op("v", [cv, "tgt"], ["dz"], V.tensor_tensor, sl("dz"), T[cv][:, 15:C:16], sl("tgt"), OP.is_equal)
             small("dw", "dz", OP.mult, "ww")
             small("dsg", "dw", OP.add, "pf")
             vcopy("sgw", "dsg")
 
-        gath(sl("smr"), "smr", sl("ssb"), "ssb", mw)
-        gath(sl("spr"), "spr", sl("smr"), "smr", "pw")
+        both("smr", "ssb", mw)
+        both("spr", "smr", "pw")
+        pback(3)
         half(0)
         op("v", ["smr", "mupw", "spr"], ["dr"], V.tensor_tensor, sl("dr"), T.smr[:, :].indirect(sl("mupw")), sl("spr"), OP.subtract)
         copy_a(sl("sg16"), ["dr"], ["sg16"], sl("dr"), func=AF.Sign)
         half(1)
-        zpart(0)
         if s < 3:
             sigma()
+            zpart(0)
             gath(sl("u16"), "u16", sl(qr), qr, "sgw")
             half(2)
             zpart(1)
-            rowlist(sl("u16"), "u16", "uw", "k16", "sc")
-            half(3)
+            rowlist(sl("u16"), "u16", "uw")
             gath(sl("sgp"), "sgp", sl("iot"), "iot", "sgw")
+            half(3)
             gath(sl("sgr"), "sgr", sl("sgp"), "sgp", "pw")
         else:
+            zpart(0)
             half(2)
             zpart(1)
             half(3)
@@ -420,14 +442,17 @@ def rank_program(g, core, T, topo):
         for b in range(4):
             op("v", [("rsb", b), mw, ("fo", b)], [("xn", b)], V.tensor_tensor, T.xn[:, b:4 * C:4], sl("rsb", b).indirect(sl(mw)), sl("fo", b), OP.add)
             if s == 3 and b == 2:
-                rowlist(sl("u16"), "u16", "uw", "k16", "sc")
+                rowlist(sl("u16"), "u16", "uw")
                 gath(row(1), slot[1], sl("sgr"), "sgr", "uw")
-    op("v", ["xn"], ["tq3", "ts3"], V.quantize_mx, sl("tq3"), sl("ts3"), sl("xn"))
-    mm(T.pb[:, 0:C], ("pb", 0), "vq", "vs", 0, "tq3", "ts3")
+    h = C // 2
+    for k in range(2):
+        op("v", ["xn"], [("tq3", k), ("ts3", k)], V.quantize_mx, T.tq3[:, h * k:h * k + h], T.ts3[:, h * k:h * k + h], T.xn[:, 4 * h * k:4 * h * k + 4 * h])
+        op("t", ["vq", "vs", ("tq3", k), ("ts3", k)], [("pb", k)], M.matmul_mx, T.pb[:, 512 * k:512 * k + h], sl("vq"), sl("vs"), T.tq3[:, h * k:h * k + h], T.ts3[:, h * k:h * k + h], True, True)
+    for k in range(2):
+        copy_a(T.ysb[:, h * k:h * k + h], [], [("ysb", k), ("pb", k)], T.pb[:, 512 * k:512 * k + h])
+        dma("a" if k else "s", "dy%d" % k, T.y[:, h * k:h * k + h], T.ysb[:, h * k:h * k + h], [("ysb", k)], [])
     dma("s", "doc", T.oc[:, :], T.tq3[:, :].bitcast(dt.uint8), ["tq3"], [])
-    copy_a(sl("ysb"), [], ["ysb", ("pb", 0)], T.pb[:, 0:C])
-    dma("a", "dy", T.y[:, :], sl("ysb"), ["ysb"], [])
-    gath(sl("qr3"), "qr3", row(1), slot[1], "pw")
+    copy_a(sl("qr3"), [slot[1], "pw"], ["qr3"], row(1).indirect(sl("pw")), bias=192.0)
     for k in range(4):
         dma("s", "dos%d" % k, T.osc[4 * k:4 * k + 4, 0:C], T.ts3[32 * k:32 * k + 4, 0:C], ["ts3"], [])
     dma("s", "dqo", T.qo[:, :], T.qr3[0:128:16, :], ["qr3"], [])

from concourse.mybir import dt, AluOpType as OP, ActivationFunctionType as AF

C = 384
HD = (1, 2, 3)
SCRATCH = {}
LISTS = ["qw", "pw", "muw", "mupw", "sgw", "uw", "ix0", "ix1", "ix2", "ix3"] + ["l%d" % n for n in (2, 4, 8, 16, 32, 64)] + ["a%d" % s for s in (1, 2, 3)] + ["m%d" % s for s in (1, 2, 3)] + ["ra%d" % s for s in (1, 2, 3)] + ["rm%d" % s for s in (1, 2, 3)]


def _sb(names, width, dtype, where="sbuf"):
    for n in names.split():
        SCRATCH[n] = (where, [128, width], dtype)


_sb("iot murow mpr sgp sgr u16 sg16 qr0 qr1 qr2", C, "bfloat16")
_sb("wlo wmi whi", 4 * 512, "bfloat16")
_sb("wtop", 7 * 512, "bfloat16")
_sb("ssb smr spr dr ysb qr3", C, "float32")
_sb("rsb", 4 * C, "float32")
_sb("mk0 mk1 sc0 sc1 k16 ka kb", C, "float16")
_sb("hf hm h0 h1 hd", C, "bfloat16")
_sb("hs gs th2 tg2", 416, "bfloat16")
_sb("th1 tg1", C, "bfloat16")
_sb("x0 xn z fo fp fa", 4 * C, "bfloat16")
_sb("ut vt ones", 512, "bfloat16")
_sb("et", 2048, "bfloat16")
_sb("eq wq", 512, "float8_e4m3fn_x4")
_sb("es wsc", 512, "uint8")
_sb("uq vq up", 128, "float8_e4m3fn_x4")
_sb("us vs ups", 128, "uint8")
_sb("tq0 tq1 tq2 tq3 lq1 lq2 lq3 zq1 zq2 zq3", C, "float8_e4m3fn_x4")
_sb("ts0 ts1 ts2 ts3 lp1 lp2 lp3 zs1 zs2 zs3", C, "uint8")
_sb("pli qli mli", 24, "int32")
_sb("ij idi", C, "int32")
_sb("pi qi", 8, "int32")
_sb("c24i u8i", 24, "int32")
_sb("cols", 8, "float32")
_sb("uoff", 8, "uint16")
AT = {}


def _wrapped(buf, names, dtype):
    names = names.split()
    for i, n in enumerate(names):
        AT[n] = (buf, 24 * i)
    _sb(buf, 24 * len(names), dtype)


_wrapped("wi", "ei ex d3i d2i d1i d0i", "int32")
_wrapped("wf", "cw pf mupf ww ep eq0 ep2 eq2 ev ne ng nw cur tgt if0 if1 if2 if3 dd du dz dw dsg pmc", "float32")
_wrapped("wl", " ".join(n for n in LISTS if n[0] != "r"), "uint16")
_wrapped("wr", " ".join(n for n in LISTS if n[0] == "r"), "uint16")
_sb("pa pb", 2048, "float32", "psum")
DMAS = ["dpl", "dql", "dml", "dx", "du_", "dv", "dwc", "dws", "doc", "dos0", "dos1", "dos2", "dos3", "dy0", "dy1", "dqo", "gap_wlo", "gap_wmi", "gap_whi", "gap_wtop"] + ["id%d" % i for i in range(5)]
SEMAPHORES = ["sv", "sa", "st", "sp", "ls"] + ["%s%d" % (k, s) for s in (1, 2, 3) for k in ("at", "aa", "am")] + DMAS


def rank_program(g, core, T, topo):
    rank = T.rank_of(core)
    if rank is None:
        return
    queue = {"v": g.vector, "a": g.scalar, "t": g.tensor, "p": g, "s": g.sync}
    count = {"sv": 0, "sa": 0, "st": 0, "sp": 0}
    own = {"v": "sv", "a": "sa", "t": "st", "p": "sp"}
    know = {q: {} for q in queue}
    then = {}
    writer, readers = {}, {}

    def merge(a, b):
        for k, v in b.items():
            if a.get(k, 0) < v:
                a[k] = v

    def meets(name, part, table):
        d = table.get(name, {})
        return [d[k] for k in d if part is None or k is None or k == part]

    def regs(xs):
        return [(x, None) if not isinstance(x, tuple) else x for x in xs]

    def waits(q, reads, writes):
        need = {}
        for n, p in reads + writes:
            for tok in meets(n, p, writer):
                need[tok[0]] = max(need.get(tok[0], 0), tok[1])
        for n, p in writes:
            for toks in meets(n, p, readers):
                for tok in toks:
                    need[tok[0]] = max(need.get(tok[0], 0), tok[1])
        for s in sorted(need):
            if know[q].get(s, 0) < need[s]:
                queue[q].wait_ge(T.sem[s], need[s])
                know[q][s] = need[s]
                merge(know[q], then.get((s, need[s]), {}))

    def note(tok, reads, writes):
        for n, p in reads:
            readers.setdefault(n, {}).setdefault(p, []).append(tok)
        for n, p in writes:
            w = writer.setdefault(n, {})
            r = readers.setdefault(n, {})
            if p is None:
                w.clear()
                r.clear()
            r[p] = []
            w[p] = tok

    def op(q, reads, writes, call, *args, **kw):
        reads, writes = regs(reads), regs(writes)
        waits(q, reads, writes)
        s = own[q]
        count[s] += 1
        then[(s, count[s])] = dict(know[q])
        call(*args, **kw).then_inc(T.sem[s], 1)
        note((s, count[s]), reads, writes)

    def dma(q, sem, out, in_, reads, writes):
        reads, writes = regs(reads), regs(writes)
        if sem not in count:
            waits(q, reads, writes)
        count[sem] = n = count.get(sem, 0) + 16
        then[(sem, n)] = dict(know[q])
        queue[q].dma_start(out, in_).then_inc(T.sem[sem], 16)
        note((sem, n), reads, writes)

    V, A, P, M = g.vector, g.scalar, g, g.tensor

    def sl(n, i=None, w=C):
        if n in AT:
            buf, o = AT[n]
            return T[buf][:, o:o + 24]
        return T[n][:, :] if i is None else T[n][:, w * i:w * i + w]

    def gath(out, oreg, win, wreg, lst):
        op("a", [wreg, lst], [oreg], A.activation, out, win.indirect(sl(lst)), AF.Copy)

    def both(out, win, lst):
        buf, o = AT[lst]
        op("v", [win, lst], [(out, 0)], V.tensor_copy, T[out][:, 0:C // 2], sl(win).indirect(T[buf][:, o:o + 12]))
        op("a", [win, lst], [(out, 1)], A.activation, T[out][:, C // 2:C], sl(win).indirect(T[buf][:, o + 12:o + 24]), AF.Copy)

    def copy_a(out, reads, writes, in_, func=AF.Copy, **kw):
        op("a", reads, writes, A.activation, out, in_, func, **kw)

    turn = [0]

    def rowlist(row, rreg, lst, col=0):
        i = turn[0] = 1 - turn[0]
        cv = "sc%d" % i
        op("v", [rreg, "k16"], [cv], V.tensor_tensor_scan, sl(cv), sl("k16"), row, 0.0, OP.add, OP.min)
        op("v", [cv, ("cols", col)], [lst], V.tensor_scalar, sl(lst), T[cv][:, 15:C:16], T.cols[:, col:col + 1], None, OP.add)

    def level(win, lst, out, dig):
        i = turn[0] = 1 - turn[0]
        mk, sc = "mk%d" % i, "sc%d" % i
        both(mk, win, lst)
        op("v", [mk, "k16"], [sc], V.tensor_tensor_scan, sl(sc), sl("k16"), sl(mk), 0.0, OP.add, OP.min)
        if dig:
            f = "if%s" % out[-1]
            op("v", [sc, dig], [f], V.tensor_tensor, sl(f), T[sc][:, 15:C:16], sl(dig), OP.add)
            op("v", [f, ("cols", 0)], [out], V.tensor_scalar, sl(out), sl(f), T.cols[:, 0:1], None, OP.add)
        else:
            op("v", [sc, ("cols", 0)], [out], V.tensor_scalar, sl(out), T[sc][:, 15:C:16], T.cols[:, 0:1], None, OP.add)

    def small(out, in0, op0, in1):
        op("v", [in0, in1], [out], V.tensor_tensor, sl(out), sl(in0), sl(in1), op0)

    def ts(out, in0, s1, s2, o0, o1, reads, writes):
        if o1 is None:
            op("v", reads, writes, V.tensor_scalar, out, in0, s1, None, o0)
        else:
            op("v", reads, writes, V.tensor_scalar, out, in0, s1, s2, o0, o1)

    def ts1(out, in0, s1, o0):
        op("v", [in0], [out], V.tensor_scalar, sl(out), sl(in0), s1, None, o0)

    def vcopy(out, in_):
        op("v", [in_], [out], V.tensor_copy, sl(out), sl(in_))

    def mm(out, oreg, lq, lqs, a, rq, rs):
        op("t", [lq, lqs, rq, rs], [oreg], M.matmul_mx, out, T[lq][:, a:a + 128], T[lqs][:, a:a + 128], sl(rq), sl(rs), True, True)

    dma("s", "dpl", sl("pli"), T.pl[:, :], [], ["pli"])
    dma("a", "dx", sl("x0"), T.x[:, :], [], ["x0"])
    dma("s", "dql", sl("qli"), T.ql[:, :], [], ["qli"])
    dma("s", "du_", sl("ut"), T.u[:, :], [], ["ut"])
    waits("s", [("x0", None)], [])
    dma("s", "dml", sl("mli"), T.ml[:, :], [], ["mli"])
    dma("s", "dwc", T.wq[:, :].bitcast(dt.uint8), T.wc[:, :], [], ["wq"])
    dma("s", "dws", sl("wsc"), T.ws[:, :], [], ["wsc"])
    dma("s", "dv", sl("vt"), T.v[:, :], [], ["vt"])

    op("p", [], ["pi"], P.iota, T.pi[:, 0:1], [[1, 1]], 0, 1)
    op("p", [], ["ij"], P.iota, sl("ij"), [[1, C]], 128, -1)
    op("p", [], ["iot"], P.iota, sl("iot"), [[1, C]], -192, 0, allow_small_or_imprecise_dtypes=True)
    op("p", [], ["u8i"], P.iota, T.u8i[:, 0:8], [[16, 8]], 0, 0)
    op("p", [], ["c24i"], P.iota, sl("c24i"), [[16, 24]], 0, 0)
    op("p", [], ["ones"], P.iota, sl("ones"), [[0, 512]], 1, 0, allow_small_or_imprecise_dtypes=True)
    for i, (w, j) in enumerate((("wlo", 0), ("wmi", 0), ("whi", 0), ("wtop", 0), ("wtop", 3))):
        dma("s", "id%d" % i, T[w][:, j * 512:j * 512 + C], sl("iot"), ["iot"], [(w, j)])
    for w, n in (("wlo", 4), ("wmi", 4), ("whi", 4), ("wtop", 7)):
        for j in range(n):
            dma("s", "gap_" + w, T[w][:, j * 512 + C:j * 512 + 512], T.ones[:, 0:128], ["ones"], [(w, "gap")])
    for b in range(4):
        op("p", ["ones"], [("et", b)], P.affine_select, sl("et", b, 512), sl("ones"), [[-1, 512]], OP.is_equal, 0.0, b, 4)
    ts(T.qi[:, 0:1], T.pi[:, 0:1], 15, None, OP.bitwise_and, None, ["pi"], [("qi", 0)])
    ts(T.cols[:, 6:7], T.qi[:, 0:1], 15, 1024.0, OP.is_lt, OP.mult, [("qi", 0)], [("cols", 6)])
    ts(T.cols[:, 0:1], T.cols[:, 6:7], 192.0, None, OP.add, None, [("cols", 6)], [("cols", 0)])
    ts1("idi", "ij", 15, OP.bitwise_and)
    ts(sl("ka"), sl("idi"), 0, 2048.0, OP.is_equal, OP.mult, ["idi"], ["ka"])
    vcopy("pw", "pli")
    vcopy("qw", "qli")
    gath(sl("qr0"), "qr0", sl("iot"), "iot", "qw")
    gath(T.wlo[:, 512:512 + C], ("wlo", 1), sl("qr0"), "qr0", "pw")
    gath(T.wtop[:, 2048:2048 + C], ("wtop", 4), sl("iot"), "iot", "pw")
    ts(sl("kb"), sl("idi"), 1, -1024.0, OP.is_equal, OP.mult, ["idi"], ["kb"])
    small("k16", "ka", OP.add, "kb")
    op("v", ["u8i"], ["uoff"], V.tensor_copy, sl("uoff"), T.u8i[:, 0:8])
    op("v", ["ut"], ["uq", "us"], V.quantize_mx, sl("uq"), sl("us"), sl("ut"))
    op("v", ["uq", "uoff"], ["up"], V.tensor_copy, T.up[:, :].bitcast(dt.uint32), T.uq[:, :].bitcast(dt.uint32).indirect(T.uoff[:, :]))
    op("v", ["us", "uoff"], ["ups"], V.tensor_copy, sl("ups"), T.us[:, :].indirect(T.uoff[:, :]))
    ts(T.qi[:, 1:2], T.pi[:, 0:1], 31, None, OP.bitwise_and, None, ["pi"], [("qi", 1)])
    ts(T.cols[:, 1:2], T.qi[:, 0:1], 8, 256.0, OP.is_lt, OP.mult, [("qi", 0)], [("cols", 1)])
    ts(T.cols[:, 2:3], T.qi[:, 0:1], 8, 256.0, OP.is_ge, OP.mult, [("qi", 0)], [("cols", 2)])

    def rest_v():
        ts(T.cols[:, 3:4], T.qi[:, 1:2], 16, 512.0, OP.is_lt, OP.mult, [("qi", 1)], [("cols", 3)])
        ts(T.cols[:, 4:5], T.qi[:, 1:2], 16, 512.0, OP.is_ge, OP.mult, [("qi", 1)], [("cols", 4)])
        ts(T.cols[:, 5:6], T.qi[:, 0:1], 0, None, OP.add, None, [("qi", 0)], [("cols", 5)])
        ts(sl("cw"), sl("c24i"), T.cols[:, 5:6], None, OP.add, None, ["c24i", ("cols", 5)], ["cw"])
        vcopy("pf", "pli")
        small("pmc", "pf", OP.subtract, "cw")
        ts1("pmc", "pmc", 2.0 ** -17, OP.mult)
        op("v", [], [("hs", 1)], V.memset, T.hs[:, 0:16], 0.0)
        op("v", [], [("hs", 2)], V.memset, T.hs[:, 400:416], 0.0)
        op("v", [], [("gs", 1)], V.memset, T.gs[:, 0:16], 0.0)
        op("v", [], [("gs", 2)], V.memset, T.gs[:, 400:416], 0.0)
        vcopy("muw", "mli")

    def rest_b():
        rowlist(sl("mpr"), "mpr", "mupf")
        vcopy("mupw", "mupf")
        small("ww", "mupf", OP.subtract, "pf")
        ts(sl("du"), sl("ww"), 0.0, 2.0, OP.is_lt, OP.mult, ["ww"], ["du"])
        ts1("dd", "du", -1.0, OP.add)
        ts(sl("tgt"), sl("dd"), T.cols[:, 6:7], None, OP.subtract, None, ["dd", ("cols", 6)], ["tgt"])
        op("v", ["vt"], ["vq", "vs"], V.quantize_mx, sl("vq"), sl("vs"), sl("vt"))

    slot = {}
    for n in (1, 2, 3):
        slot[n], slot[4 * n], slot[16 * n] = ("wlo", n), ("wmi", n), ("whi", n)
    slot[64], slot[128], slot["p"], slot["p64"], slot["p128"] = [("wtop", i) for i in (1, 2, 4, 5, 6)]

    def row(n):
        w, i = slot[n]
        return T[w][:, 512 * i:512 * i + C]

    def lname(s, n):
        return "a%d" % s if n == 1 else "l%d" % n

    def power(s, to, n, by):
        gath(row(to), slot[to], row(n), slot[n], lname(s, by))

    def chain_row(s, i):
        power(s, 2 << i, 1 << i, 1 << i)

    def chain_list(s, i):
        rowlist(row(2 << i), slot[2 << i], lname(s, 2 << i))

    send_n = [0]

    def send(s, dst, sem, out, in_, reads):
        waits("p", regs(reads), [])
        rid, pid, _ = topo.addr(dst)
        g.remote_dma(out, in_, T.sem[sem], T.sem.ls, pid, rid, topo.mask(core, dst))
        send_n[0] += len(topo.engines(core, dst))

    steps = T.tables["STEP"] if "STEP" in T.tables else [1, 2, 3]
    for s in (1, 2, 3):
        dst = T.cores[rank ^ steps[s - 1]]
        ne = len(topo.engines(core, dst))
        tq, tsn, lq, lp = "tq%d" % (s - 1), "ts%d" % (s - 1), "lq%d" % s, "lp%d" % s
        xin = "x0" if s == 1 else "xn"
        mw, rm, ra = "m%d" % s, "rm%d" % s, "ra%d" % s
        op("v", [xin], [tq, tsn], V.quantize_mx, sl(tq), sl(tsn), sl(xin))
        mm(T.pb[:, 0:C], ("pb", 0), "up", "ups", 0, tq, tsn)
        send(s, dst, "at%d" % s, T[lq][:, :].bitcast(dt.uint8), T[tq][:, :].bitcast(dt.uint8), [tq])
        send(s, dst, "at%d" % s, sl(lp), sl(tsn), [tsn])
        if s == 1:
            rowlist(row(1), slot[1], "a1")
            chain_row(1, 0)
        send(s, dst, "aa%d" % s, sl(ra), sl("a%d" % s), ["a%d" % s])
        for tok, names in ((("at%d" % s, 2 * ne), [lq, lp]), (("aa%d" % s, ne), [ra]), (("am%d" % s, ne), [rm])):
            count[tok[0]] = tok[1]
            note(tok, [], regs(names))
        if s > 1:
            chain_list(s, 0)
        ts(sl("hm"), T.pb[:, 0:C], 0.0, T.cols[:, 2:3], OP.is_ge, OP.mult, [("cols", 2)], ["hm", ("pb", 0)])
        ts(sl("hf"), T.pb[:, 0:C], 0.0, T.cols[:, 1:2], OP.is_ge, OP.mult, [("cols", 1)], ["hf", ("pb", 0)])
        if s == 1:
            chain_list(s, 0)
        op("v", ["hm", "pw", "hf"], ["h0"], V.tensor_tensor, sl("h0"), T.hm[:, :].indirect(sl("pw")), sl("hf"), OP.add)

        def unpack():
            for b in range(4):
                mm(T.pa[:, 512 * b:512 * b + C], ("pa", b), "eq", "es", 128 * b, tq, tsn)
            for b in range(1, 4):
                mm(T.pb[:, 512 * b:512 * b + C], ("pb", b), "eq", "es", 128 * b, lq, lp)

        jobs = [(0, lambda: copy_a(sl("ssb"), [], ["ssb", ("pb", 0)], T.pb[:, 0:C]))]
        if s == 1:
            jobs.append((1, rest_v))
            jobs.append((2, lambda: op("v", ["et"], ["eq", "es"], V.quantize_mx, sl("eq"), sl("es"), sl("et"))))
            jobs.append((2, unpack))
            jobs.append((3, lambda: gath(sl("murow"), "murow", sl("iot"), "iot", "muw")))
            jobs.append((4, lambda: gath(sl("mpr"), "mpr", sl("murow"), "murow", "pw")))
        else:
            unpack()
        jobs.append((3, lambda: power(s, 3, 1, 2)))
        jobs.append((4, lambda: power(s, 12, 4, 8)))
        for b in range(4):
            jobs.append((5, lambda b=b: copy_a(sl("fo", b), [], [("fo", b), ("pa", b)], T.pa[:, 512 * b:512 * b + C])))
        jobs += [(5, lambda: power(s, 48, 16, 32)), (6, lambda: power(s, 128, 64, 64)), (6, lambda: power(s, "p64", "p", 64))]

        def some(i, k):
            while jobs and k and jobs[0][0] <= i:
                jobs.pop(0)[1]()
                k -= 1

        cur = "h0"
        for i, n in enumerate((1, 2, 4, 8, 16, 32, 64, 64)):
            if i in HD:
                copy_a(sl("hd"), [cur], ["hd"], sl(cur), bias=float(-n))
            else:
                ts(sl("hd"), sl(cur), float(-n), None, OP.add, None, [cur], ["hd"])
            if i < 5:
                chain_row(s, i + 1)
            some(i, (1, 3, 3, 1, 1, 2, 2, 2)[i])
            nxt = "h1" if cur == "h0" else "h0"
            oreg, out = (nxt, sl(nxt)) if i < 7 else (("hs", 0), T.hs[:, 16:16 + C])
            op("v", [cur, lname(s, n), "hd"], [oreg], V.tensor_tensor, out, T[cur][:, :].indirect(sl(lname(s, n))), sl("hd"), OP.min)
            if i < 5:
                chain_list(s, i + 1)
            cur = nxt

        def pback(b):
            copy_a(sl("fp", b), [], [("fp", b), ("pb", b)], T.pb[:, 512 * b:512 * b + C], scale=0.5)

        gath(T.gs[:, 16:16 + C], ("gs", 0), T.hs[:, 16:16 + C], "hs", "pw")
        op("v", ["hs"], ["th1"], V.transpose, sl("th1"), T.hs[:, 16:16 + C])
        op("v", ["hs"], ["th2"], V.transpose, sl("th2"), sl("hs"))
        some(9, 99)
        mm(T.pb[:, 0:C], ("pb", 0), "eq", "es", 0, lq, lp)
        op("v", ["gs"], ["tg1"], V.transpose, sl("tg1"), T.gs[:, 16:16 + C])
        op("v", ["gs"], ["tg2"], V.transpose, sl("tg2"), sl("gs"))
        for out, k, a, a0, a1, b, b0, b1 in (("ep", 0, "th1", 0, 384, "tg1", 8, 384), ("eq0", 1, "th1", 16, 384, "tg1", 24, 384), ("eq0", 0, "th2", 16, 400, "tg2", 24, 400), ("ep", 1, "th2", 32, 416, "tg2", 40, 416)):
            op("v", [a, b], [(out, k)], V.tensor_tensor, T[AT[out][0]][:, AT[out][1] + k:AT[out][1] + 24:2], T[a][:, a0:a1:32], T[b][:, b0:b1:32], OP.subtract)
        ts(sl("ep2"), sl("ep"), T.cols[:, 3:4], None, OP.mult, None, ["ep", ("cols", 3)], ["ep2"])
        ts(sl("eq2"), sl("eq0"), T.cols[:, 4:5], None, OP.mult, None, ["eq0", ("cols", 4)], ["eq2"])
        small("ev", "ep2", OP.add, "eq2")
        ts1("ne", "ev", -1.0, OP.mult)
        ts(sl("ng"), sl("ev"), 0.0, 131072.0, OP.is_lt, OP.mult, ["ev"], ["ng"])
        small("ei", "ev", OP.max, "ne")
        small("nw", "ng", OP.mult, "pmc")
        ts1("d0i", "ei", 1536, OP.bitwise_and)
        small("cur", "nw", OP.add, "cw")
        ts(sl("d1i"), sl("ei"), 2, 1536, OP.logical_shift_right, OP.bitwise_and, ["ei"], ["d1i"])
        small("if0", "d0i", OP.add, "cur")
        ts(sl("d2i"), sl("ei"), 4, 1536, OP.logical_shift_right, OP.bitwise_and, ["ei"], ["d2i"])
        vcopy("ix0", "if0")
        level("wlo", "ix0", "ix1", "d1i")
        power(s, "p128", "p64", 64)
        small("ex", "ei", OP.add, "ng")
        level("wmi", "ix1", "ix2", "d2i")
        pback(0)
        ts(sl("d3i"), sl("ex"), 6, 3584, OP.logical_shift_right, OP.bitwise_and, ["ex"], ["d3i"])
        level("whi", "ix2", "ix3", "d3i")
        pback(1)
        level("wtop", "ix3", mw, None)
        send(s, dst, "am%d" % s, sl(rm), sl(mw), [mw])
        pback(2)
        if s == 1:
            rest_b()
        qr, zq, zs = "qr%d" % (s - 1), "zq%d" % s, "zs%d" % s

        def half(b):
            gath(sl("fa", b), ("fa", b), sl("fp", b), ("fp", b), ra)

        def zpart(b):
            op("v", [("fp", b), rm, ("fa", b)], [("z", b)], V.tensor_tensor, T.z[:, b:4 * C:4], sl("fp", b).indirect(sl(rm)), sl("fa", b), OP.add)

        def sigma():
            i = turn[0] = 1 - turn[0]
            cv = "sc%d" % i
            op("v", ["sg16", "k16"], [cv], V.tensor_tensor_scan, sl(cv), sl("k16"), sl("sg16"), 0.0, OP.add, OP.min)
            op("v", [cv, "tgt"], ["dz"], V.tensor_tensor, sl("dz"), T[cv][:, 15:C:16], sl("tgt"), OP.is_equal)
            small("dw", "dz", OP.mult, "ww")
            small("dsg", "dw", OP.add, "pf")
            vcopy("sgw", "dsg")

        both("smr", "ssb", mw)
        both("spr", "smr", "pw")
        pback(3)
        half(0)
        op("v", ["smr", "mupw", "spr"], ["dr"], V.tensor_tensor, sl("dr"), T.smr[:, :].indirect(sl("mupw")), sl("spr"), OP.subtract)
        copy_a(sl("sg16"), ["dr"], ["sg16"], sl("dr"), func=AF.Sign)
        half(1)
        if s < 3:
            sigma()
            zpart(0)
            gath(sl("u16"), "u16", sl(qr), qr, "sgw")
            half(2)
            zpart(1)
            rowlist(sl("u16"), "u16", "uw")
            gath(sl("sgp"), "sgp", sl("iot"), "iot", "sgw")
            half(3)
            gath(sl("sgr"), "sgr", sl("sgp"), "sgp", "pw")
        else:
            zpart(0)
            half(2)
            zpart(1)
            half(3)
        zpart(2)
        zpart(3)
        op("v", ["z"], [zq, zs], V.quantize_mx, sl(zq), sl(zs), sl("z"))
        for b in range(4):
            mm(T.pa[:, 512 * b:512 * b + C], ("pa", b), "wq", "wsc", 128 * b, zq, zs)
        if s < 3:
            gath(row(1), slot[1], sl("sgr"), "sgr", "uw")
        else:
            sigma()
        for b in range(4):
            copy_a(sl("rsb", b), [], [("rsb", b), ("pa", b)], T.pa[:, 512 * b:512 * b + C], scale=0.03125)
            if b == 2 and s < 3:
                rowlist(row(1), slot[1], "a%d" % (s + 1))
                chain_row(s + 1, 0)
        if s == 3:
            gath(sl("u16"), "u16", sl(qr), qr, "sgw")
            gath(sl("sgp"), "sgp", sl("iot"), "iot", "sgw")
            gath(sl("sgr"), "sgr", sl("sgp"), "sgp", "pw")
        else:
            gath(sl("qr%d" % s), "qr%d" % s, row(1), slot[1], "pw")
        for b in range(4):
            op("v", [("rsb", b), mw, ("fo", b)], [("xn", b)], V.tensor_tensor, T.xn[:, b:4 * C:4], sl("rsb", b).indirect(sl(mw)), sl("fo", b), OP.add)
            if s == 3 and b == 2:
                rowlist(sl("u16"), "u16", "uw")
                gath(row(1), slot[1], sl("sgr"), "sgr", "uw")
    h = C // 2
    for k in range(2):
        op("v", ["xn"], [("tq3", k), ("ts3", k)], V.quantize_mx, T.tq3[:, h * k:h * k + h], T.ts3[:, h * k:h * k + h], T.xn[:, 4 * h * k:4 * h * k + 4 * h])
        op("t", ["vq", "vs", ("tq3", k), ("ts3", k)], [("pb", k)], M.matmul_mx, T.pb[:, 512 * k:512 * k + h], sl("vq"), sl("vs"), T.tq3[:, h * k:h * k + h], T.ts3[:, h * k:h * k + h], True, True)
    for k in range(2):
        copy_a(T.ysb[:, h * k:h * k + h], [], [("ysb", k), ("pb", k)], T.pb[:, 512 * k:512 * k + h])
        dma("a" if k else "s", "dy%d" % k, T.y[:, h * k:h * k + h], T.ysb[:, h * k:h * k + h], [("ysb", k)], [])
    dma("s", "doc", T.oc[:, :], T.tq3[:, :].bitcast(dt.uint8), ["tq3"], [])
    copy_a(sl("qr3"), [slot[1], "pw"], ["qr3"], row(1).indirect(sl("pw")), bias=192.0)
    for k in range(4):
        dma("s", "dos%d" % k, T.osc[4 * k:4 * k + 4, 0:C], T.ts3[32 * k:32 * k + 4, 0:C], ["ts3"], [])
    dma("s", "dqo", T.qo[:, :], T.qr3[0:128:16, :], ["qr3"], [])
    for sem in sorted(count):
        if know["p"].get(sem, 0) < count[sem]:
            g.wait_ge(T.sem[sem], count[sem])
    g.wait_ge(T.sem.ls, send_n[0])
